import numpy as np
import ml_dtypes


def mxq(x, axis, fmt="e4m3"):
    dtype, down = {"e4m3": (ml_dtypes.float8_e4m3fn, 7), "e5m2": (ml_dtypes.float8_e5m2, 14)}[fmt]
    v = np.moveaxis(np.asarray(x, np.float32).astype(ml_dtypes.bfloat16).astype(np.float64), axis, -1)
    blocks = v.reshape(v.shape[:-1] + (-1, 32))
    amax = np.abs(blocks).max(-1, keepdims=True)
    byte = np.maximum(np.where(amax > 0, np.frexp(amax)[1] - 1 + 127, 0) - down, 1)
    scale = np.exp2(byte - 127.0)
    codes = (blocks / scale).astype(np.float32).astype(dtype).astype(np.float64)
    return np.moveaxis((codes * scale).reshape(v.shape), -1, axis)


WIDE = False


def mx_kscale(k):
    if not WIDE:
        return np.ones(k)
    levels = np.array([10, -10, 5, -5, 0])
    if k % 512:
        return np.exp2(np.random.permutation(np.resize(levels, k // 32))).repeat(32)
    a = np.empty((k // 512, 16))
    for p in range(k // 512):
        a[p, :8] = np.random.permutation(np.resize(levels, 8))
        for g in range(8):
            far = levels[np.abs(levels - a[p, g]) >= 10]
            a[p, g + 8] = far[np.random.randint(len(far))]
    return np.exp2(a.ravel()).repeat(32)


def f64(x):
    return np.asarray(x).astype(np.float64)


def striped8(idx):
    return np.concatenate([v.reshape(-1, 16).T for v in idx]).astype(np.uint16)


def unstriped8(offs):
    return np.stack([offs[16 * g:16 * g + 16].T.reshape(-1) for g in range(8)]).astype(np.int64)


G, K, M, T, S = 4, 1024, 128, 2048, 256


def setup_inputs():
    n = np.random.standard_normal
    s = mx_kscale(K)[:, None]
    return {
        "xT": (n((K, T)) * s).astype(np.float32),
        "w": (n((K, M)) / np.sqrt(K) / s).astype(np.float32),
        "wgt": np.repeat(np.random.uniform(0.5, 2.0, (8, G * S)), 16, axis=0).astype(np.float32),
        "r": (n((256, 128))).astype(np.float32),
        "offs": striped8(np.stack([np.concatenate([np.random.permutation(T)[:S] for _ in range(G)]) for _ in range(8)])),
    }


def reference(xT, w, wgt, r, offs):
    idx = unstriped8(offs)
    group = np.arange(K) % 512 // 64
    xg = f64(wgt)[np.arange(K) // 4 % 128] * f64(xT)[np.arange(K)[:, None], idx[group]]
    xT_ = mxq(xg, 0, "e4m3")
    xT_ = xT_.reshape(K, G, S).sum(1)
    w_ = mxq(f64(w), 0, "e4m3")
    y = xT_.T @ w_
    return f64(r) + y

@@ -1,0 +1,135 @@
+from contextlib import ExitStack
+
+import concourse.mybir as mybir
+
+G, K, M, T, S = 4, 1024, 128, 2048, 256
+FLOPS = 2 * K * G * S * M
+
+F32 = mybir.dt.float32
+BF16 = mybir.dt.bfloat16
+U32 = mybir.dt.uint32
+U16 = mybir.dt.uint16
+U8 = mybir.dt.uint8
+FP8X4 = mybir.dt.float8_e4m3fn_x4
+MULT = mybir.AluOpType.mult
+ADD = mybir.AluOpType.add
+
+P = 128
+PACK = 4
+PASSES = K // (P * PACK)
+PICKS = G * S
+HALF = PICKS // 2
+LIST_ROWS = 16
+
+
+def tile_list_hbag_tm_res_kernel(tc, xT, w, wgt, r, offs, out):
+    nc = tc.nc
+    with ExitStack() as ctx:
+        held = ctx.enter_context(tc.tile_pool(name="held", bufs=1))
+        psum = ctx.enter_context(tc.psum_pool(name="psum", bufs=1))
+
+        offsets = held.tile([P, PICKS // LIST_ROWS], U16, name="offsets")
+        wgt_sb = [held.tile([P, HALF], F32, name="wgt%d" % h) for h in range(2)]
+        planes = [held.tile([P, T], F32, name="plane%d" % q) for q in range(PASSES * PACK)]
+        w_raw = held.tile([P, PASSES, PACK, M], F32, name="w_raw")
+        r_sb = held.tile([P, 2, M], F32, name="r_sb")
+        x_rows = xT.rearrange("(a p i) t -> a i p t", p=P, i=PACK)
+
+        def load_plane(q):
+            nc.sync.dma_start(planes[q][:], x_rows[q // PACK, q % PACK])
+
+        nc.sync.dma_start(offsets[:], offs)
+        nc.sync.dma_start(wgt_sb[0][:], wgt[:, 0:HALF])
+        load_plane(0)
+        nc.sync.dma_start(wgt_sb[1][:], wgt[:, HALF:PICKS])
+        for q in range(1, 5):
+            load_plane(q)
+        nc.sync.dma_start(w_raw[:], w.rearrange("(a p i) n -> p a i n", p=P, i=PACK))
+        for q in range(5, 8):
+            load_plane(q)
+        nc.sync.dma_start(r_sb[:], r.rearrange("(h p) n -> p h n", p=P))
+
+        picked = [held.tile([P, 2, PICKS], F32, name="picked%d" % u) for u in range(2 * PASSES)]
+        grouped = [held.tile([P, PICKS, PACK], BF16, name="grouped%d" % a, align_bytes=64) for a in range(PASSES)]
+        x_codes = [held.tile([P, PICKS], U32, name="x_codes%d" % a, align_bytes=64) for a in range(PASSES)]
+        x_scales = [held.tile([P, PICKS], U8, name="x_scales%d" % a, align_bytes=64) for a in range(PASSES)]
+        w_grouped = held.tile([P, PASSES, M, PACK], BF16, name="w_grouped", align_bytes=64)
+        w_codes = held.tile([P, PASSES * M], U32, name="w_codes", align_bytes=64)
+        w_scales = held.tile([P, PASSES * M], U8, name="w_scales", align_bytes=64)
+        acc = [psum.tile([P, M], F32, name="acc%d" % h) for h in range(2)]
+        result = [held.tile([P, M], F32, name="result%d" % h) for h in range(2)]
+
+        def gather(q, lo, hi):
+            h = lo // HALF
+            nc.vector.tensor_tensor(
+                picked[q // 2][:, q % 2, lo:hi],
+                planes[q][:].indirect(offsets[:, lo // LIST_ROWS : hi // LIST_ROWS]),
+                wgt_sb[h][:, lo - h * HALF : hi - h * HALF],
+                MULT,
+            )
+
+        def interleave(u, lo, hi):
+            i0 = 2 * (u % 2)
+            nc.scalar.copy(
+                grouped[u // 2][:, lo:hi, i0 : i0 + 2],
+                picked[u][:, :, lo:hi].rearrange("p i n -> p n i"),
+            )
+
+        def multiply(a, lo, hi):
+            for m0 in range(lo, hi, P):
+                h = (m0 // P) % 2
+                nc.tensor.matmul_mx(
+                    out=acc[h][:],
+                    lhsT=x_codes[a][:, m0 : m0 + P].bitcast(FP8X4),
+                    lhsT_scale=x_scales[a][:, m0 : m0 + P],
+                    rhs=w_codes[:, a * M : (a + 1) * M].bitcast(FP8X4),
+                    rhs_scale=w_scales[:, a * M : (a + 1) * M],
+                    start=(a == 0 and m0 < S),
+                    stop=(a == PASSES - 1 and m0 >= PICKS - S),
+                )
+
+        def quantize(a, lo, hi):
+            nc.vector.quantize_mx(
+                out=x_codes[a][:, lo:hi].bitcast(FP8X4),
+                scales=x_scales[a][:, lo:hi],
+                in_=grouped[a][:, lo:hi, :].rearrange("p n i -> p (n i)"),
+            )
+
+        def finish(h):
+            nc.vector.tensor_tensor(result[h][:], acc[h][:], r_sb[:, h, :], ADD)
+            nc.sync.dma_start(out[h * P : (h + 1) * P, :], result[h][:])
+
+        halves = [(0, HALF), (HALF, PICKS)]
+        for q in range(4):
+            for lo, hi in halves:
+                gather(q, lo, hi)
+                if q % 2 == 1:
+                    interleave(q // 2, lo, hi)
+        for a in range(PASSES):
+            nc.scalar.copy(
+                w_grouped[:, a, :, :].rearrange("p (c e) i -> p c i e", e=4),
+                w_raw[:, a, :, :].rearrange("p i (c e) -> p c i e", e=4),
+            )
+        for lo, hi in halves:
+            gather(4, lo, hi)
+            quantize(0, lo, hi)
+        for lo, hi in halves:
+            gather(5, lo, hi)
+            interleave(2, lo, hi)
+        nc.vector.quantize_mx(
+            out=w_codes[:].bitcast(FP8X4),
+            scales=w_scales[:],
+            in_=w_grouped[:].rearrange("p a n i -> p (a n i)"),
+        )
+        multiply(0, 0, PICKS)
+        for lo, hi in halves:
+            gather(6, lo, hi)
+        tail = [(0, 256), (256, 512), (512, 768), (768, 896), (896, 1024)]
+        for lo, hi in tail:
+            gather(7, lo, hi)
+            interleave(3, lo, hi)
+        for lo, hi in tail:
+            quantize(1, lo, hi)
+            multiply(1, lo, hi)
+        finish(0)
+        finish(1)

@@ -49,7 +49,7 @@ def tile_list_hbag_tm_res_kernel(tc, xT, w, wgt, r, offs, out):
             load_plane(q)
         nc.sync.dma_start(r_sb[:], r.rearrange("(h p) n -> p h n", p=P))
 
-        picked = [held.tile([P, 2, PICKS], F32, name="picked%d" % u) for u in range(2 * PASSES)]
+        picked = [held.tile([P, PACK, PICKS], F32, name="picked%d" % a) for a in range(PASSES)]
         grouped = [held.tile([P, PICKS, PACK], BF16, name="grouped%d" % a, align_bytes=64) for a in range(PASSES)]
         x_codes = [held.tile([P, PICKS], U32, name="x_codes%d" % a, align_bytes=64) for a in range(PASSES)]
         x_scales = [held.tile([P, PICKS], U8, name="x_scales%d" % a, align_bytes=64) for a in range(PASSES)]
@@ -62,20 +62,19 @@ def tile_list_hbag_tm_res_kernel(tc, xT, w, wgt, r, offs, out):
         def gather(q, lo, hi):
             h = lo // HALF
             nc.vector.tensor_tensor(
-                picked[q // 2][:, q % 2, lo:hi],
+                picked[q // PACK][:, q % PACK, lo:hi],
                 planes[q][:].indirect(offsets[:, lo // LIST_ROWS : hi // LIST_ROWS]),
                 wgt_sb[h][:, lo - h * HALF : hi - h * HALF],
                 MULT,
             )
 
-        def interleave(u, lo, hi):
-            i0 = 2 * (u % 2)
-            nc.scalar.copy(
-                grouped[u // 2][:, lo:hi, i0 : i0 + 2],
-                picked[u][:, :, lo:hi].rearrange("p i n -> p n i"),
+        def interleave(copy, a, lo, hi):
+            copy(
+                grouped[a][:, lo:hi, :].rearrange("p (c e) i -> p c i e", e=4),
+                picked[a][:, :, lo:hi].rearrange("p i (c e) -> p c i e", e=4),
             )
 
-        def multiply(a, lo, hi):
+        def multiply(a, lo, hi, last=False):
             for m0 in range(lo, hi, P):
                 h = (m0 // P) % 2
                 nc.tensor.matmul_mx(
@@ -85,7 +84,7 @@ def tile_list_hbag_tm_res_kernel(tc, xT, w, wgt, r, offs, out):
                     rhs=w_codes[:, a * M : (a + 1) * M].bitcast(FP8X4),
                     rhs_scale=w_scales[:, a * M : (a + 1) * M],
                     start=(a == 0 and m0 < S),
-                    stop=(a == PASSES - 1 and m0 >= PICKS - S),
+                    stop=last,
                 )
 
         def quantize(a, lo, hi):
@@ -100,36 +99,43 @@ def tile_list_hbag_tm_res_kernel(tc, xT, w, wgt, r, offs, out):
             nc.sync.dma_start(out[h * P : (h + 1) * P, :], result[h][:])
 
         halves = [(0, HALF), (HALF, PICKS)]
+        quarters = [(c * S, (c + 1) * S) for c in range(G)]
         for q in range(4):
             for lo, hi in halves:
                 gather(q, lo, hi)
-                if q % 2 == 1:
-                    interleave(q // 2, lo, hi)
+                if q == 3:
+                    interleave(nc.scalar.copy, 0, lo, hi)
         for a in range(PASSES):
             nc.scalar.copy(
                 w_grouped[:, a, :, :].rearrange("p (c e) i -> p c i e", e=4),
                 w_raw[:, a, :, :].rearrange("p i (c e) -> p c i e", e=4),
             )
-        for lo, hi in halves:
-            gather(4, lo, hi)
-            quantize(0, lo, hi)
-        for lo, hi in halves:
-            gather(5, lo, hi)
-            interleave(2, lo, hi)
+        gather(4, 0, HALF)
+        gather(4, HALF, PICKS)
+        quantize(0, 0, HALF)
+        gather(5, 0, HALF)
+        gather(5, HALF, PICKS)
+        quantize(0, HALF, PICKS)
+        gather(6, 0, HALF)
         nc.vector.quantize_mx(
             out=w_codes[:].bitcast(FP8X4),
             scales=w_scales[:],
             in_=w_grouped[:].rearrange("p a n i -> p (a n i)"),
         )
         multiply(0, 0, PICKS)
-        for lo, hi in halves:
-            gather(6, lo, hi)
-        tail = [(0, 256), (256, 512), (512, 768), (768, 896), (896, 1024)]
-        for lo, hi in tail:
+        gather(6, HALF, PICKS)
+        for lo, hi in quarters:
             gather(7, lo, hi)
-            interleave(3, lo, hi)
-        for lo, hi in tail:
-            quantize(1, lo, hi)
-            multiply(1, lo, hi)
+        for lo, hi in quarters[:3]:
+            interleave(nc.scalar.copy, 1, lo, hi)
+        quantize(1, 0, S)
+        multiply(1, 0, S, False)
+        interleave(nc.vector.tensor_copy, 1, 3 * S, 4 * S)
+        quantize(1, S, 2 * S)
+        multiply(1, S, 2 * S, False)
+        quantize(1, 3 * S, 4 * S)
+        multiply(1, 3 * S, 4 * S, False)
+        quantize(1, 2 * S, 3 * S)
+        multiply(1, 2 * S, 3 * S, True)
         finish(0)
         finish(1)

@@ -1,6 +1,7 @@
 from contextlib import ExitStack
 
 import concourse.mybir as mybir
+from concourse.masks import make_identity
 
 G, K, M, T, S = 4, 1024, 128, 2048, 256
 FLOPS = 2 * K * G * S * M
@@ -20,6 +21,7 @@ PASSES = K // (P * PACK)
 PICKS = G * S
 HALF = PICKS // 2
 LIST_ROWS = 16
+LISTS = P // LIST_ROWS
 
 
 def tile_list_hbag_tm_res_kernel(tc, xT, w, wgt, r, offs, out):
@@ -29,7 +31,9 @@ def tile_list_hbag_tm_res_kernel(tc, xT, w, wgt, r, offs, out):
         psum = ctx.enter_context(tc.psum_pool(name="psum", bufs=1))
 
         offsets = held.tile([P, PICKS // LIST_ROWS], U16, name="offsets")
-        wgt_sb = [held.tile([P, HALF], F32, name="wgt%d" % h) for h in range(2)]
+        wgt_parts = [(0, 256), (256, 512), (512, 1024)]
+        wgt_sb = held.tile([P, PICKS], F32, name="wgt_sb")
+        wgt_rows = held.tile([P, P], F32, name="wgt_rows")
         planes = [held.tile([P, T], F32, name="plane%d" % q) for q in range(PASSES * PACK)]
         w_raw = held.tile([P, PASSES, PACK, M], F32, name="w_raw")
         r_sb = held.tile([P, 2, M], F32, name="r_sb")
@@ -38,10 +42,12 @@ def tile_list_hbag_tm_res_kernel(tc, xT, w, wgt, r, offs, out):
         def load_plane(q):
             nc.sync.dma_start(planes[q][:], x_rows[q // PACK, q % PACK])
 
-        nc.sync.dma_start(offsets[:], offs)
-        nc.sync.dma_start(wgt_sb[0][:], wgt[:, 0:HALF])
+        nc.sync.dma_start(
+            wgt_rows[:], wgt.rearrange("(y r) (b c) -> r y b c", r=8, c=P)[0]
+        )
         load_plane(0)
-        nc.sync.dma_start(wgt_sb[1][:], wgt[:, HALF:PICKS])
+        nc.sync.dma_start(offsets[:], offs)
+        nc.sync.dma_start(wgt_sb[:, 0:S], wgt[:, 0:S])
         for q in range(1, 5):
             load_plane(q)
         nc.sync.dma_start(w_raw[:], w.rearrange("(a p i) n -> p a i n", p=P, i=PACK))
@@ -49,7 +55,34 @@ def tile_list_hbag_tm_res_kernel(tc, xT, w, wgt, r, offs, out):
             load_plane(q)
         nc.sync.dma_start(r_sb[:], r.rearrange("(h p) n -> p h n", p=P))
 
-        picked = [held.tile([P, PACK, PICKS], F32, name="picked%d" % a) for a in range(PASSES)]
+        ident = held.tile([P, P], F32, name="ident")
+        make_identity(nc, ident[:])
+        turned = psum.tile([P, LISTS, LIST_ROWS], F32, name="turned")
+        nc.tensor.transpose(turned[:].rearrange("p g x -> p (g x)"), wgt_rows[:], ident[:])
+        backs = []
+        for lo, hi in wgt_parts[1:]:
+            b0, b1 = lo // P, hi // P
+            wide = held.tile([P, b1 - b0, LISTS, LIST_ROWS], F32, name="wide%d" % lo)
+            nc.scalar.copy(
+                wide[:],
+                turned[:, :, b0:b1].rearrange("p g b -> p b g").unsqueeze(3).to_broadcast([P, b1 - b0, LISTS, LIST_ROWS]),
+            )
+            back = psum.tile([P, b1 - b0, P], F32, name="back%d" % lo)
+            for b in range(b1 - b0):
+                nc.tensor.transpose(back[:, b, :], wide[:, b, :, :].rearrange("p g x -> p (g x)"), ident[:])
+            backs.append(back)
+        for (lo, hi), back in zip(wgt_parts[1:], backs):
+            nc.scalar.copy(wgt_sb[:, lo:hi], back[:].rearrange("p b c -> p (b c)"))
+
+        picked = [held.tile([P, 2, PICKS], F32, name="picked%d" % u) for u in range(3)]
+        picked.append(held.tile([P, 2, 896], F32, name="picked3"))
+
+        def spot(u, lo, hi):
+            if u < 3:
+                return slice(lo, hi)
+            shift = 896 - 640 if lo < 640 else -640
+            return slice(lo + shift, hi + shift)
+
         grouped = [held.tile([P, PICKS, PACK], BF16, name="grouped%d" % a, align_bytes=64) for a in range(PASSES)]
         x_codes = [held.tile([P, PICKS], U32, name="x_codes%d" % a, align_bytes=64) for a in range(PASSES)]
         x_scales = [held.tile([P, PICKS], U8, name="x_scales%d" % a, align_bytes=64) for a in range(PASSES)]
@@ -58,23 +91,24 @@ def tile_list_hbag_tm_res_kernel(tc, xT, w, wgt, r, offs, out):
         w_scales = held.tile([P, PASSES * M], U8, name="w_scales", align_bytes=64)
         acc = [psum.tile([P, M], F32, name="acc%d" % h) for h in range(2)]
         result = [held.tile([P, M], F32, name="result%d" % h) for h in range(2)]
+        done = [0, 0]
 
         def gather(q, lo, hi):
-            h = lo // HALF
             nc.vector.tensor_tensor(
-                picked[q // PACK][:, q % PACK, lo:hi],
+                picked[q // 2][:, q % 2, spot(q // 2, lo, hi)],
                 planes[q][:].indirect(offsets[:, lo // LIST_ROWS : hi // LIST_ROWS]),
-                wgt_sb[h][:, lo - h * HALF : hi - h * HALF],
+                wgt_sb[:, lo:hi],
                 MULT,
             )
 
-        def interleave(copy, a, lo, hi):
+        def pair(copy, u, lo, hi):
+            i0 = 2 * (u % 2)
             copy(
-                grouped[a][:, lo:hi, :].rearrange("p (c e) i -> p c i e", e=4),
-                picked[a][:, :, lo:hi].rearrange("p i (c e) -> p c i e", e=4),
+                grouped[u // 2][:, lo:hi, i0 : i0 + 2],
+                picked[u][:, :, spot(u, lo, hi)].rearrange("p i n -> p n i"),
             )
 
-        def multiply(a, lo, hi, last=False):
+        def multiply(a, lo, hi):
             for m0 in range(lo, hi, P):
                 h = (m0 // P) % 2
                 nc.tensor.matmul_mx(
@@ -83,9 +117,10 @@ def tile_list_hbag_tm_res_kernel(tc, xT, w, wgt, r, offs, out):
                     lhsT_scale=x_scales[a][:, m0 : m0 + P],
                     rhs=w_codes[:, a * M : (a + 1) * M].bitcast(FP8X4),
                     rhs_scale=w_scales[:, a * M : (a + 1) * M],
-                    start=(a == 0 and m0 < S),
-                    stop=last,
+                    start=(done[h] == 0),
+                    stop=(done[h] == PASSES * G - 1),
                 )
+                done[h] += 1
 
         def quantize(a, lo, hi):
             nc.vector.quantize_mx(
@@ -94,48 +129,56 @@ def tile_list_hbag_tm_res_kernel(tc, xT, w, wgt, r, offs, out):
                 in_=grouped[a][:, lo:hi, :].rearrange("p n i -> p (n i)"),
             )
 
-        def finish(h):
-            nc.vector.tensor_tensor(result[h][:], acc[h][:], r_sb[:, h, :], ADD)
-            nc.sync.dma_start(out[h * P : (h + 1) * P, :], result[h][:])
+        def prepare_w():
+            for a in range(PASSES):
+                nc.scalar.copy(
+                    w_grouped[:, a, :, :].rearrange("p (c e) i -> p c i e", e=4),
+                    w_raw[:, a, :, :].rearrange("p i (c e) -> p c i e", e=4),
+                )
 
-        halves = [(0, HALF), (HALF, PICKS)]
-        quarters = [(c * S, (c + 1) * S) for c in range(G)]
-        for q in range(4):
-            for lo, hi in halves:
-                gather(q, lo, hi)
-                if q == 3:
-                    interleave(nc.scalar.copy, 0, lo, hi)
-        for a in range(PASSES):
-            nc.scalar.copy(
-                w_grouped[:, a, :, :].rearrange("p (c e) i -> p c i e", e=4),
-                w_raw[:, a, :, :].rearrange("p i (c e) -> p c i e", e=4),
+        def quantize_w():
+            nc.vector.quantize_mx(
+                out=w_codes[:].bitcast(FP8X4),
+                scales=w_scales[:],
+                in_=w_grouped[:].rearrange("p a n i -> p (a n i)"),
             )
-        gather(4, 0, HALF)
-        gather(4, HALF, PICKS)
-        quantize(0, 0, HALF)
-        gather(5, 0, HALF)
-        gather(5, HALF, PICKS)
-        quantize(0, HALF, PICKS)
-        gather(6, 0, HALF)
-        nc.vector.quantize_mx(
-            out=w_codes[:].bitcast(FP8X4),
-            scales=w_scales[:],
-            in_=w_grouped[:].rearrange("p a n i -> p (a n i)"),
-        )
-        multiply(0, 0, PICKS)
-        gather(6, HALF, PICKS)
-        for lo, hi in quarters:
+
+        def finish(h, queue):
+            nc.vector.tensor_tensor(result[h][:], acc[h][:], r_sb[:, h, :], ADD)
+            queue.dma_start(out[h * P : (h + 1) * P, :], result[h][:])
+
+        act = nc.scalar.copy
+        dve = nc.vector.tensor_copy
+        gather(0, 0, 256)
+        gather(0, 256, 512)
+        gather(0, 512, 1024)
+        for lo, hi in ((0, 768), (768, 1024)):
+            gather(1, lo, hi)
+            pair(act, 0, lo, hi)
+        gather(2, 0, 768)
+        gather(2, 768, 1024)
+        for lo, hi in ((0, 512), (512, 1024)):
+            gather(3, lo, hi)
+            pair(act, 1, lo, hi)
+        prepare_w()
+        gather(4, 0, 512)
+        gather(4, 512, 1024)
+        quantize(0, 0, 512)
+        quantize(0, 512, 1024)
+        for lo, hi in ((0, 256), (256, 640), (640, 1024)):
+            gather(5, lo, hi)
+            pair(act, 2, lo, hi)
+        quantize_w()
+        multiply(0, 0, 1024)
+        gather(6, 0, 640)
+        tail = ((0, 128), (128, 384), (384, 640), (640, 896), (896, 1024))
+        for lo, hi in tail:
+            if lo == 640:
+                gather(6, 640, 1024)
             gather(7, lo, hi)
-        for lo, hi in quarters[:3]:
-            interleave(nc.scalar.copy, 1, lo, hi)
-        quantize(1, 0, S)
-        multiply(1, 0, S, False)
-        interleave(nc.vector.tensor_copy, 1, 3 * S, 4 * S)
-        quantize(1, S, 2 * S)
-        multiply(1, S, 2 * S, False)
-        quantize(1, 3 * S, 4 * S)
-        multiply(1, 3 * S, 4 * S, False)
-        quantize(1, 2 * S, 3 * S)
-        multiply(1, 2 * S, 3 * S, True)
-        finish(0)
-        finish(1)
+            pair(act, 3, lo, hi)
+        for lo, hi in tail:
+            quantize(1, lo, hi)
+            multiply(1, lo, hi)
+        finish(0, nc.sync)
+        finish(1, nc.sync)

@@ -31,7 +31,7 @@ def tile_list_hbag_tm_res_kernel(tc, xT, w, wgt, r, offs, out):
         psum = ctx.enter_context(tc.psum_pool(name="psum", bufs=1))
 
         offsets = held.tile([P, PICKS // LIST_ROWS], U16, name="offsets")
-        wgt_parts = [(0, 256), (256, 512), (512, 1024)]
+        wgt_parts = [(0, 128), (128, 384), (768, 1024), (384, 768)]
         wgt_sb = held.tile([P, PICKS], F32, name="wgt_sb")
         wgt_rows = held.tile([P, P], F32, name="wgt_rows")
         planes = [held.tile([P, T], F32, name="plane%d" % q) for q in range(PASSES * PACK)]
@@ -47,7 +47,6 @@ def tile_list_hbag_tm_res_kernel(tc, xT, w, wgt, r, offs, out):
         )
         load_plane(0)
         nc.sync.dma_start(offsets[:], offs)
-        nc.sync.dma_start(wgt_sb[:, 0:S], wgt[:, 0:S])
         for q in range(1, 5):
             load_plane(q)
         nc.sync.dma_start(w_raw[:], w.rearrange("(a p i) n -> p a i n", p=P, i=PACK))
@@ -57,22 +56,24 @@ def tile_list_hbag_tm_res_kernel(tc, xT, w, wgt, r, offs, out):
 
         ident = held.tile([P, P], F32, name="ident")
         make_identity(nc, ident[:])
-        turned = psum.tile([P, LISTS, LIST_ROWS], F32, name="turned")
-        nc.tensor.transpose(turned[:].rearrange("p g x -> p (g x)"), wgt_rows[:], ident[:])
+        movers = [nc.vector.tensor_copy, nc.scalar.copy, nc.scalar.copy, nc.scalar.copy]
+        turned = [psum.tile([P, LISTS, LIST_ROWS], F32, name="turned%d" % e) for e in range(2)]
+        for e in range(2):
+            nc.tensor.transpose(turned[e][:].rearrange("p g x -> p (g x)"), wgt_rows[:], ident[:])
         backs = []
-        for lo, hi in wgt_parts[1:]:
+        for j, (lo, hi) in enumerate(wgt_parts):
             b0, b1 = lo // P, hi // P
             wide = held.tile([P, b1 - b0, LISTS, LIST_ROWS], F32, name="wide%d" % lo)
-            nc.scalar.copy(
+            movers[j](
                 wide[:],
-                turned[:, :, b0:b1].rearrange("p g b -> p b g").unsqueeze(3).to_broadcast([P, b1 - b0, LISTS, LIST_ROWS]),
+                turned[min(j, 1)][:, :, b0:b1].rearrange("p g b -> p b g").unsqueeze(3).to_broadcast([P, b1 - b0, LISTS, LIST_ROWS]),
             )
             back = psum.tile([P, b1 - b0, P], F32, name="back%d" % lo)
             for b in range(b1 - b0):
                 nc.tensor.transpose(back[:, b, :], wide[:, b, :, :].rearrange("p g x -> p (g x)"), ident[:])
             backs.append(back)
-        for (lo, hi), back in zip(wgt_parts[1:], backs):
-            nc.scalar.copy(wgt_sb[:, lo:hi], back[:].rearrange("p b c -> p (b c)"))
+        for j, (lo, hi) in enumerate(wgt_parts):
+            movers[j](wgt_sb[:, lo:hi], backs[j][:].rearrange("p b c -> p (b c)"))
 
         picked = [held.tile([P, 2, PICKS], F32, name="picked%d" % u) for u in range(3)]
         picked.append(held.tile([P, 2, 896], F32, name="picked3"))
@@ -149,14 +150,13 @@ def tile_list_hbag_tm_res_kernel(tc, xT, w, wgt, r, offs, out):
 
         act = nc.scalar.copy
         dve = nc.vector.tensor_copy
-        gather(0, 0, 256)
-        gather(0, 256, 512)
-        gather(0, 512, 1024)
-        for lo, hi in ((0, 768), (768, 1024)):
+        for lo, hi in wgt_parts:
+            gather(0, lo, hi)
+        for lo, hi in ((0, 512), (512, 1024)):
             gather(1, lo, hi)
             pair(act, 0, lo, hi)
-        gather(2, 0, 768)
-        gather(2, 768, 1024)
+        gather(2, 0, 512)
+        gather(2, 512, 1024)
         for lo, hi in ((0, 512), (512, 1024)):
             gather(3, lo, hi)
             pair(act, 1, lo, hi)

@@ -47,10 +47,10 @@ def tile_list_hbag_tm_res_kernel(tc, xT, w, wgt, r, offs, out):
         )
         load_plane(0)
         nc.sync.dma_start(offsets[:], offs)
-        for q in range(1, 5):
+        for q in range(1, 6):
             load_plane(q)
         nc.sync.dma_start(w_raw[:], w.rearrange("(a p i) n -> p a i n", p=P, i=PACK))
-        for q in range(5, 8):
+        for q in range(6, 8):
             load_plane(q)
         nc.sync.dma_start(r_sb[:], r.rearrange("(h p) n -> p h n", p=P))
 
@@ -84,12 +84,11 @@ def tile_list_hbag_tm_res_kernel(tc, xT, w, wgt, r, offs, out):
             shift = 896 - 640 if lo < 640 else -640
             return slice(lo + shift, hi + shift)
 
-        grouped = [held.tile([P, PICKS, PACK], BF16, name="grouped%d" % a, align_bytes=64) for a in range(PASSES)]
-        x_codes = [held.tile([P, PICKS], U32, name="x_codes%d" % a, align_bytes=64) for a in range(PASSES)]
-        x_scales = [held.tile([P, PICKS], U8, name="x_scales%d" % a, align_bytes=64) for a in range(PASSES)]
-        w_grouped = held.tile([P, PASSES, M, PACK], BF16, name="w_grouped", align_bytes=64)
-        w_codes = held.tile([P, PASSES * M], U32, name="w_codes", align_bytes=64)
-        w_scales = held.tile([P, PASSES * M], U8, name="w_scales", align_bytes=64)
+        x0 = PASSES * M
+        cols = x0 + PASSES * PICKS
+        grouped = held.tile([P, cols, PACK], BF16, name="grouped", align_bytes=64)
+        codes = held.tile([P, cols], U32, name="codes", align_bytes=64)
+        scales = held.tile([P, cols], U8, name="scales", align_bytes=64)
         acc = [psum.tile([P, M], F32, name="acc%d" % h) for h in range(2)]
         result = [held.tile([P, M], F32, name="result%d" % h) for h in range(2)]
         done = [0, 0]
@@ -105,80 +104,70 @@ def tile_list_hbag_tm_res_kernel(tc, xT, w, wgt, r, offs, out):
         def pair(copy, u, lo, hi):
             i0 = 2 * (u % 2)
             copy(
-                grouped[u // 2][:, lo:hi, i0 : i0 + 2],
+                grouped[:, x0 + (u // 2) * PICKS + lo : x0 + (u // 2) * PICKS + hi, i0 : i0 + 2],
                 picked[u][:, :, spot(u, lo, hi)].rearrange("p i n -> p n i"),
             )
 
         def multiply(a, lo, hi):
             for m0 in range(lo, hi, P):
                 h = (m0 // P) % 2
+                c0 = x0 + a * PICKS + m0
                 nc.tensor.matmul_mx(
                     out=acc[h][:],
-                    lhsT=x_codes[a][:, m0 : m0 + P].bitcast(FP8X4),
-                    lhsT_scale=x_scales[a][:, m0 : m0 + P],
-                    rhs=w_codes[:, a * M : (a + 1) * M].bitcast(FP8X4),
-                    rhs_scale=w_scales[:, a * M : (a + 1) * M],
+                    lhsT=codes[:, c0 : c0 + P].bitcast(FP8X4),
+                    lhsT_scale=scales[:, c0 : c0 + P],
+                    rhs=codes[:, a * M : (a + 1) * M].bitcast(FP8X4),
+                    rhs_scale=scales[:, a * M : (a + 1) * M],
                     start=(done[h] == 0),
                     stop=(done[h] == PASSES * G - 1),
                 )
                 done[h] += 1
 
-        def quantize(a, lo, hi):
+        def quantize(lo, hi):
             nc.vector.quantize_mx(
-                out=x_codes[a][:, lo:hi].bitcast(FP8X4),
-                scales=x_scales[a][:, lo:hi],
-                in_=grouped[a][:, lo:hi, :].rearrange("p n i -> p (n i)"),
+                out=codes[:, lo:hi].bitcast(FP8X4),
+                scales=scales[:, lo:hi],
+                in_=grouped[:, lo:hi, :].rearrange("p n i -> p (n i)"),
             )
 
         def prepare_w():
             for a in range(PASSES):
                 nc.scalar.copy(
-                    w_grouped[:, a, :, :].rearrange("p (c e) i -> p c i e", e=4),
+                    grouped[:, a * M : (a + 1) * M, :].rearrange("p (c e) i -> p c i e", e=4),
                     w_raw[:, a, :, :].rearrange("p i (c e) -> p c i e", e=4),
                 )
-
-        def quantize_w():
-            nc.vector.quantize_mx(
-                out=w_codes[:].bitcast(FP8X4),
-                scales=w_scales[:],
-                in_=w_grouped[:].rearrange("p a n i -> p (a n i)"),
-            )
 
         def finish(h, queue):
             nc.vector.tensor_tensor(result[h][:], acc[h][:], r_sb[:, h, :], ADD)
             queue.dma_start(out[h * P : (h + 1) * P, :], result[h][:])
 
         act = nc.scalar.copy
-        dve = nc.vector.tensor_copy
         for lo, hi in wgt_parts:
             gather(0, lo, hi)
-        for lo, hi in ((0, 512), (512, 1024)):
-            gather(1, lo, hi)
-            pair(act, 0, lo, hi)
-        gather(2, 0, 512)
-        gather(2, 512, 1024)
-        for lo, hi in ((0, 512), (512, 1024)):
-            gather(3, lo, hi)
-            pair(act, 1, lo, hi)
+        gather(1, 0, PICKS)
+        pair(act, 0, 0, PICKS)
+        gather(2, 0, PICKS)
+        gather(3, 0, PICKS)
+        pair(act, 1, 768, PICKS)
+        pair(act, 1, 0, 768)
+        gather(4, 0, PICKS)
+        gather(5, 0, PICKS)
         prepare_w()
-        gather(4, 0, 512)
-        gather(4, 512, 1024)
-        quantize(0, 0, 512)
-        quantize(0, 512, 1024)
-        for lo, hi in ((0, 256), (256, 640), (640, 1024)):
-            gather(5, lo, hi)
-            pair(act, 2, lo, hi)
-        quantize_w()
-        multiply(0, 0, 1024)
+        pair(act, 2, 0, PICKS)
+        quantize(x0 + 768, x0 + PICKS)
+        quantize(0, x0 + 768)
+        multiply(0, 0, PICKS)
         gather(6, 0, 640)
-        tail = ((0, 128), (128, 384), (384, 640), (640, 896), (896, 1024))
-        for lo, hi in tail:
+        for lo, hi in ((0, 384), (384, 640), (640, 896), (896, 1024)):
             if lo == 640:
                 gather(6, 640, 1024)
             gather(7, lo, hi)
+            if lo == 0:
+                pair(act, 3, 0, 128)
+                lo = 128
             pair(act, 3, lo, hi)
-        for lo, hi in tail:
-            quantize(1, lo, hi)
+        for lo, hi in ((0, 512), (512, 768), (768, 896), (896, 1024)):
+            quantize(x0 + PICKS + lo, x0 + PICKS + hi)
             multiply(1, lo, hi)
         finish(0, nc.sync)
         finish(1, nc.sync)

@@ -35,7 +35,7 @@ def tile_list_hbag_tm_res_kernel(tc, xT, w, wgt, r, offs, out):
         wgt_sb = held.tile([P, PICKS], F32, name="wgt_sb")
         wgt_rows = held.tile([P, P], F32, name="wgt_rows")
         planes = [held.tile([P, T], F32, name="plane%d" % q) for q in range(PASSES * PACK)]
-        w_raw = held.tile([P, PASSES, PACK, M], F32, name="w_raw")
+        w_raw = held.tile([P, PASSES, PACK, M], F32, name="w_raw", tag="late", align_bytes=64)
         r_sb = held.tile([P, 2, M], F32, name="r_sb")
         x_rows = xT.rearrange("(a p i) t -> a i p t", p=P, i=PACK)
 
@@ -86,7 +86,8 @@ def tile_list_hbag_tm_res_kernel(tc, xT, w, wgt, r, offs, out):
 
         x0 = PASSES * M
         cols = x0 + PASSES * PICKS
-        grouped = held.tile([P, cols, PACK], BF16, name="grouped", align_bytes=64)
+        grouped = [held.tile([P, x0 + PICKS, PACK], BF16, name="grouped0", align_bytes=64)]
+        first = [0, x0 + PICKS]
         codes = held.tile([P, cols], U32, name="codes", align_bytes=64)
         scales = held.tile([P, cols], U8, name="scales", align_bytes=64)
         acc = [psum.tile([P, M], F32, name="acc%d" % h) for h in range(2)]
@@ -103,8 +104,9 @@ def tile_list_hbag_tm_res_kernel(tc, xT, w, wgt, r, offs, out):
 
         def pair(copy, u, lo, hi):
             i0 = 2 * (u % 2)
+            c0 = x0 if u < 2 else 0
             copy(
-                grouped[:, x0 + (u // 2) * PICKS + lo : x0 + (u // 2) * PICKS + hi, i0 : i0 + 2],
+                grouped[u // 2][:, c0 + lo : c0 + hi, i0 : i0 + 2],
                 picked[u][:, :, spot(u, lo, hi)].rearrange("p i n -> p n i"),
             )
 
@@ -124,16 +126,17 @@ def tile_list_hbag_tm_res_kernel(tc, xT, w, wgt, r, offs, out):
                 done[h] += 1
 
         def quantize(lo, hi):
+            a = 0 if lo < first[1] else 1
             nc.vector.quantize_mx(
                 out=codes[:, lo:hi].bitcast(FP8X4),
                 scales=scales[:, lo:hi],
-                in_=grouped[:, lo:hi, :].rearrange("p n i -> p (n i)"),
+                in_=grouped[a][:, lo - first[a] : hi - first[a], :].rearrange("p n i -> p (n i)"),
             )
 
         def prepare_w():
             for a in range(PASSES):
                 nc.scalar.copy(
-                    grouped[:, a * M : (a + 1) * M, :].rearrange("p (c e) i -> p c i e", e=4),
+                    grouped[0][:, a * M : (a + 1) * M, :].rearrange("p (c e) i -> p c i e", e=4),
                     w_raw[:, a, :, :].rearrange("p i (c e) -> p c i e", e=4),
                 )
 
@@ -151,23 +154,35 @@ def tile_list_hbag_tm_res_kernel(tc, xT, w, wgt, r, offs, out):
         pair(act, 1, 768, PICKS)
         pair(act, 1, 0, 768)
         gather(4, 0, PICKS)
-        gather(5, 0, PICKS)
+        gather(5, 0, 384)
         prepare_w()
-        pair(act, 2, 0, PICKS)
+        grouped.append(held.tile([P, PICKS, PACK], BF16, name="grouped1", tag="late", align_bytes=64))
+        pair(act, 2, 0, 384)
+        gather(5, 384, PICKS)
+        pair(act, 2, 384, PICKS)
         quantize(x0 + 768, x0 + PICKS)
         quantize(0, x0 + 768)
         multiply(0, 0, PICKS)
-        gather(6, 0, 640)
-        for lo, hi in ((0, 384), (384, 640), (640, 896), (896, 1024)):
-            if lo == 640:
-                gather(6, 640, 1024)
-            gather(7, lo, hi)
-            if lo == 0:
-                pair(act, 3, 0, 128)
-                lo = 128
-            pair(act, 3, lo, hi)
-        for lo, hi in ((0, 512), (512, 768), (768, 896), (896, 1024)):
+        def close(lo, hi):
             quantize(x0 + PICKS + lo, x0 + PICKS + hi)
             multiply(1, lo, hi)
+
+        gather(6, 0, 640)
+        gather(7, 0, 256)
+        pair(act, 3, 0, 128)
+        pair(act, 3, 128, 256)
+        gather(7, 256, 640)
+        pair(act, 3, 256, 640)
+        gather(6, 640, 1024)
+        gather(7, 640, 768)
+        pair(act, 3, 640, 768)
+        gather(7, 768, 1024)
+        pair(act, 3, 768, 896)
+        pair(act, 3, 896, 1024)
+        close(0, 256)
+        close(256, 512)
+        close(512, 768)
+        close(768, 896)
+        close(896, 1024)
         finish(0, nc.sync)
         finish(1, nc.sync)

@@ -18,10 +18,17 @@ ADD = mybir.AluOpType.add
 P = 128
 PACK = 4
 PASSES = K // (P * PACK)
+PLANES = PASSES * PACK
 PICKS = G * S
-HALF = PICKS // 2
 LIST_ROWS = 16
 LISTS = P // LIST_ROWS
+BLOCKS = PICKS // P
+HALVES = S // P
+
+WGT_PARTS = (1, 2, 2, 3)
+PLANES_BEFORE_W = 6
+PLANE5_CUT = 3 * P
+PLANE6_CUT = 5 * P
 
 
 def tile_list_hbag_tm_res_kernel(tc, xT, w, wgt, r, offs, out):
@@ -31,158 +38,148 @@ def tile_list_hbag_tm_res_kernel(tc, xT, w, wgt, r, offs, out):
         psum = ctx.enter_context(tc.psum_pool(name="psum", bufs=1))
 
         offsets = held.tile([P, PICKS // LIST_ROWS], U16, name="offsets")
-        wgt_parts = [(0, 128), (128, 384), (768, 1024), (384, 768)]
         wgt_sb = held.tile([P, PICKS], F32, name="wgt_sb")
         wgt_rows = held.tile([P, P], F32, name="wgt_rows")
-        planes = [held.tile([P, T], F32, name="plane%d" % q) for q in range(PASSES * PACK)]
-        w_raw = held.tile([P, PASSES, PACK, M], F32, name="w_raw", tag="late", align_bytes=64)
-        r_sb = held.tile([P, 2, M], F32, name="r_sb")
+        planes = [held.tile([P, T], F32, name="plane%d" % q) for q in range(PLANES)]
+        w_raw = held.tile([P, PASSES, PACK, M], F32, name="w_raw", tag="w_then_pass1", align_bytes=64)
+        r_sb = held.tile([P, HALVES, M], F32, name="r_sb")
         x_rows = xT.rearrange("(a p i) t -> a i p t", p=P, i=PACK)
 
         def load_plane(q):
             nc.sync.dma_start(planes[q][:], x_rows[q // PACK, q % PACK])
 
-        nc.sync.dma_start(
-            wgt_rows[:], wgt.rearrange("(y r) (b c) -> r y b c", r=8, c=P)[0]
-        )
+        half_rows = wgt.rearrange("p (e b c) -> (p e) b c", e=2, c=P)
+        nc.sync.dma_start(wgt_rows[: LISTS * BLOCKS, :], half_rows[:: LIST_ROWS + 1])
         load_plane(0)
         nc.sync.dma_start(offsets[:], offs)
-        for q in range(1, 6):
+        for q in range(1, PLANES_BEFORE_W):
             load_plane(q)
         nc.sync.dma_start(w_raw[:], w.rearrange("(a p i) n -> p a i n", p=P, i=PACK))
-        for q in range(6, 8):
+        for q in range(PLANES_BEFORE_W, PLANES):
             load_plane(q)
         nc.sync.dma_start(r_sb[:], r.rearrange("(h p) n -> p h n", p=P))
 
+        nc.vector.memset(wgt_rows[LISTS * BLOCKS :, :], 0.0)
         ident = held.tile([P, P], F32, name="ident")
         make_identity(nc, ident[:])
-        movers = [nc.vector.tensor_copy, nc.scalar.copy, nc.scalar.copy, nc.scalar.copy]
-        turned = [psum.tile([P, LISTS, LIST_ROWS], F32, name="turned%d" % e) for e in range(2)]
+        turned = [psum.tile([P, P], F32, name="turned%d" % e) for e in range(2)]
         for e in range(2):
-            nc.tensor.transpose(turned[e][:].rearrange("p g x -> p (g x)"), wgt_rows[:], ident[:])
-        backs = []
-        for j, (lo, hi) in enumerate(wgt_parts):
-            b0, b1 = lo // P, hi // P
-            wide = held.tile([P, b1 - b0, LISTS, LIST_ROWS], F32, name="wide%d" % lo)
-            movers[j](
-                wide[:],
-                turned[min(j, 1)][:, :, b0:b1].rearrange("p g b -> p b g").unsqueeze(3).to_broadcast([P, b1 - b0, LISTS, LIST_ROWS]),
-            )
-            back = psum.tile([P, b1 - b0, P], F32, name="back%d" % lo)
-            for b in range(b1 - b0):
-                nc.tensor.transpose(back[:, b, :], wide[:, b, :, :].rearrange("p g x -> p (g x)"), ident[:])
-            backs.append(back)
-        for j, (lo, hi) in enumerate(wgt_parts):
-            movers[j](wgt_sb[:, lo:hi], backs[j][:].rearrange("p b c -> p (b c)"))
+            nc.tensor.transpose(turned[e][:], wgt_rows[:], ident[:])
+        wgt_parts = []
+        for j, width in enumerate(WGT_PARTS):
+            b0 = sum(WGT_PARTS[:j])
+            by_vector = j == 0
+            move = nc.vector.tensor_copy if by_vector else nc.scalar.copy
+            by_block = turned[0 if by_vector else 1][:, : LISTS * BLOCKS].rearrange("c (g b) -> c b g", b=BLOCKS)
+            wide = held.tile([P, width, LISTS, LIST_ROWS], F32, name="wide%d" % j)
+            move(wide[:], by_block[:, b0 : b0 + width, :].unsqueeze(3).to_broadcast([P, width, LISTS, LIST_ROWS]))
+            back = psum.tile([P, width, P], F32, name="back%d" % j)
+            for b in range(width):
+                nc.tensor.transpose(back[:, b, :], wide[:, b, :, :].rearrange("c g x -> c (g x)"), ident[:])
+            wgt_parts.append((b0 * P, (b0 + width) * P, move, back))
+        for lo, hi, move, back in wgt_parts:
+            move(wgt_sb[:, lo:hi], back[:].rearrange("p b c -> p (b c)"))
 
-        picked = [held.tile([P, 2, PICKS], F32, name="picked%d" % u) for u in range(3)]
-        picked.append(held.tile([P, 2, 896], F32, name="picked3"))
+        last_pair = PLANES // 2 - 1
+        short = PICKS - P
+        picked = [held.tile([P, 2, PICKS], F32, name="picked%d" % u) for u in range(last_pair)]
+        picked.append(held.tile([P, 2, short], F32, name="picked%d" % last_pair))
 
-        def spot(u, lo, hi):
-            if u < 3:
+        def columns_of(u, lo, hi):
+            if u < last_pair:
                 return slice(lo, hi)
-            shift = 896 - 640 if lo < 640 else -640
+            shift = short - PLANE6_CUT if lo < PLANE6_CUT else -PLANE6_CUT
             return slice(lo + shift, hi + shift)
 
-        x0 = PASSES * M
-        cols = x0 + PASSES * PICKS
-        grouped = [held.tile([P, x0 + PICKS, PACK], BF16, name="grouped0", align_bytes=64)]
-        first = [0, x0 + PICKS]
-        codes = held.tile([P, cols], U32, name="codes", align_bytes=64)
-        scales = held.tile([P, cols], U8, name="scales", align_bytes=64)
-        acc = [psum.tile([P, M], F32, name="acc%d" % h) for h in range(2)]
-        result = [held.tile([P, M], F32, name="result%d" % h) for h in range(2)]
-        done = [0, 0]
+        x_at = [PASSES * M + a * PICKS for a in range(PASSES)]
+        grouped_at = [0, x_at[1]]
+        grouped = [held.tile([P, x_at[1], PACK], BF16, name="grouped0", align_bytes=64)]
+        codes = held.tile([P, x_at[1] + PICKS], U32, name="codes", align_bytes=64)
+        scales = held.tile([P, x_at[1] + PICKS], U8, name="scales", align_bytes=64)
+        acc = [psum.tile([P, M], F32, name="acc%d" % h) for h in range(HALVES)]
+        result = [held.tile([P, M], F32, name="result%d" % h) for h in range(HALVES)]
 
         def gather(q, lo, hi):
             nc.vector.tensor_tensor(
-                picked[q // 2][:, q % 2, spot(q // 2, lo, hi)],
+                picked[q // 2][:, q % 2, columns_of(q // 2, lo, hi)],
                 planes[q][:].indirect(offsets[:, lo // LIST_ROWS : hi // LIST_ROWS]),
                 wgt_sb[:, lo:hi],
                 MULT,
             )
 
-        def pair(copy, u, lo, hi):
-            i0 = 2 * (u % 2)
-            c0 = x0 if u < 2 else 0
-            copy(
-                grouped[u // 2][:, c0 + lo : c0 + hi, i0 : i0 + 2],
-                picked[u][:, :, spot(u, lo, hi)].rearrange("p i n -> p n i"),
+        def interleave(u, lo, hi):
+            a, i0 = u // 2, 2 * (u % 2)
+            c0 = x_at[a] - grouped_at[a]
+            nc.scalar.copy(
+                grouped[a][:, c0 + lo : c0 + hi, i0 : i0 + 2],
+                picked[u][:, :, columns_of(u, lo, hi)].rearrange("p i m -> p m i"),
+            )
+
+        def interleave_w(a):
+            nc.scalar.copy(
+                grouped[0][:, a * M : (a + 1) * M, :].rearrange("p (n e) i -> p n i e", e=4),
+                w_raw[:, a, :, :].rearrange("p i (n e) -> p n i e", e=4),
+            )
+
+        def quantize(a, lo, hi):
+            nc.vector.quantize_mx(
+                out=codes[:, lo:hi].bitcast(FP8X4),
+                scales=scales[:, lo:hi],
+                in_=grouped[a][:, lo - grouped_at[a] : hi - grouped_at[a], :].rearrange("p m i -> p (m i)"),
             )
 
         def multiply(a, lo, hi):
-            for m0 in range(lo, hi, P):
-                h = (m0 // P) % 2
-                c0 = x0 + a * PICKS + m0
+            for b in range(lo // P, hi // P):
+                c0 = x_at[a] + b * P
                 nc.tensor.matmul_mx(
-                    out=acc[h][:],
+                    out=acc[b % HALVES][:],
                     lhsT=codes[:, c0 : c0 + P].bitcast(FP8X4),
                     lhsT_scale=scales[:, c0 : c0 + P],
                     rhs=codes[:, a * M : (a + 1) * M].bitcast(FP8X4),
                     rhs_scale=scales[:, a * M : (a + 1) * M],
-                    start=(done[h] == 0),
-                    stop=(done[h] == PASSES * G - 1),
-                )
-                done[h] += 1
-
-        def quantize(lo, hi):
-            a = 0 if lo < first[1] else 1
-            nc.vector.quantize_mx(
-                out=codes[:, lo:hi].bitcast(FP8X4),
-                scales=scales[:, lo:hi],
-                in_=grouped[a][:, lo - first[a] : hi - first[a], :].rearrange("p n i -> p (n i)"),
-            )
-
-        def prepare_w():
-            for a in range(PASSES):
-                nc.scalar.copy(
-                    grouped[0][:, a * M : (a + 1) * M, :].rearrange("p (c e) i -> p c i e", e=4),
-                    w_raw[:, a, :, :].rearrange("p i (c e) -> p c i e", e=4),
+                    start=(a == 0 and b // HALVES == 0),
+                    stop=(a == PASSES - 1 and b // HALVES == G - 1),
                 )
 
-        def finish(h, queue):
-            nc.vector.tensor_tensor(result[h][:], acc[h][:], r_sb[:, h, :], ADD)
-            queue.dma_start(out[h * P : (h + 1) * P, :], result[h][:])
-
-        act = nc.scalar.copy
-        for lo, hi in wgt_parts:
+        quarter = PICKS - PICKS // 4
+        for lo, hi, move, back in wgt_parts:
             gather(0, lo, hi)
         gather(1, 0, PICKS)
-        pair(act, 0, 0, PICKS)
+        interleave(0, 0, PICKS)
         gather(2, 0, PICKS)
         gather(3, 0, PICKS)
-        pair(act, 1, 768, PICKS)
-        pair(act, 1, 0, 768)
+        interleave(1, quarter, PICKS)
+        interleave(1, 0, quarter)
+
         gather(4, 0, PICKS)
-        gather(5, 0, 384)
-        prepare_w()
-        grouped.append(held.tile([P, PICKS, PACK], BF16, name="grouped1", tag="late", align_bytes=64))
-        pair(act, 2, 0, 384)
-        gather(5, 384, PICKS)
-        pair(act, 2, 384, PICKS)
-        quantize(x0 + 768, x0 + PICKS)
-        quantize(0, x0 + 768)
+        gather(5, 0, PLANE5_CUT)
+        for a in range(PASSES):
+            interleave_w(a)
+        grouped.append(held.tile([P, PICKS, PACK], BF16, name="grouped1", tag="w_then_pass1", align_bytes=64))
+        interleave(2, 0, PLANE5_CUT)
+        gather(5, PLANE5_CUT, PICKS)
+        interleave(2, PLANE5_CUT, PICKS)
+        quantize(0, x_at[0] + quarter, x_at[1])
+        quantize(0, 0, x_at[0] + quarter)
         multiply(0, 0, PICKS)
-        def close(lo, hi):
-            quantize(x0 + PICKS + lo, x0 + PICKS + hi)
+
+        gather(6, 0, PLANE6_CUT)
+        gather(7, 0, 2 * P)
+        interleave(last_pair, 0, P)
+        interleave(last_pair, P, 2 * P)
+        gather(7, 2 * P, PLANE6_CUT)
+        interleave(last_pair, 2 * P, PLANE6_CUT)
+        gather(6, PLANE6_CUT, PICKS)
+        gather(7, PLANE6_CUT, PLANE6_CUT + P)
+        interleave(last_pair, PLANE6_CUT, PLANE6_CUT + P)
+        gather(7, PLANE6_CUT + P, PICKS)
+        for lo in range(PLANE6_CUT + P, PICKS, P):
+            interleave(last_pair, lo, lo + P)
+        cuts = list(range(0, PICKS - P, 2 * P)) + [PICKS - P, PICKS]
+        for lo, hi in zip(cuts, cuts[1:]):
+            quantize(1, x_at[1] + lo, x_at[1] + hi)
             multiply(1, lo, hi)
 
-        gather(6, 0, 640)
-        gather(7, 0, 256)
-        pair(act, 3, 0, 128)
-        pair(act, 3, 128, 256)
-        gather(7, 256, 640)
-        pair(act, 3, 256, 640)
-        gather(6, 640, 1024)
-        gather(7, 640, 768)
-        pair(act, 3, 640, 768)
-        gather(7, 768, 1024)
-        pair(act, 3, 768, 896)
-        pair(act, 3, 896, 1024)
-        close(0, 256)
-        close(256, 512)
-        close(512, 768)
-        close(768, 896)
-        close(896, 1024)
-        finish(0, nc.sync)
-        finish(1, nc.sync)
+        for h in range(HALVES):
+            nc.vector.tensor_tensor(result[h][:], acc[h][:], r_sb[:, h, :], ADD)
+            nc.sync.dma_start(out[h * P : (h + 1) * P, :], result[h][:])

@@ -1,7 +1,6 @@
 from contextlib import ExitStack
 
 import concourse.mybir as mybir
-from concourse.masks import make_identity
 
 G, K, M, T, S = 4, 1024, 128, 2048, 256
 FLOPS = 2 * K * G * S * M
@@ -25,7 +24,8 @@ LISTS = P // LIST_ROWS
 BLOCKS = PICKS // P
 HALVES = S // P
 
-WGT_PARTS = (1, 2, 2, 3)
+SQ = 32
+WGT_PARTS = 4
 PLANES_BEFORE_W = 6
 PLANE5_CUT = 3 * P
 PLANE6_CUT = 5 * P
@@ -38,8 +38,8 @@ def tile_list_hbag_tm_res_kernel(tc, xT, w, wgt, r, offs, out):
         psum = ctx.enter_context(tc.psum_pool(name="psum", bufs=1))
 
         offsets = held.tile([P, PICKS // LIST_ROWS], U16, name="offsets")
-        wgt_sb = held.tile([P, PICKS], F32, name="wgt_sb")
-        wgt_rows = held.tile([P, P], F32, name="wgt_rows")
+        wgt_sb = held.tile([P, PICKS], F32, name="wgt_sb", align_bytes=64)
+        wgt_rows = held.tile([P, 2 * SQ], F32, name="wgt_rows", align_bytes=64)
         planes = [held.tile([P, T], F32, name="plane%d" % q) for q in range(PLANES)]
         w_raw = held.tile([P, PASSES, PACK, M], F32, name="w_raw", tag="w_then_pass1", align_bytes=64)
         r_sb = held.tile([P, HALVES, M], F32, name="r_sb")
@@ -48,8 +48,8 @@ def tile_list_hbag_tm_res_kernel(tc, xT, w, wgt, r, offs, out):
         def load_plane(q):
             nc.sync.dma_start(planes[q][:], x_rows[q // PACK, q % PACK])
 
-        half_rows = wgt.rearrange("p (e b c) -> (p e) b c", e=2, c=P)
-        nc.sync.dma_start(wgt_rows[: LISTS * BLOCKS, :], half_rows[:: LIST_ROWS + 1])
+        half_rows = wgt.rearrange("p (e b c) -> (p e) b c", e=2, c=2 * SQ)
+        nc.sync.dma_start(wgt_rows[:], half_rows[:: LIST_ROWS + 1])
         load_plane(0)
         nc.sync.dma_start(offsets[:], offs)
         for q in range(1, PLANES_BEFORE_W):
@@ -59,26 +59,20 @@ def tile_list_hbag_tm_res_kernel(tc, xT, w, wgt, r, offs, out):
             load_plane(q)
         nc.sync.dma_start(r_sb[:], r.rearrange("(h p) n -> p h n", p=P))
 
-        nc.vector.memset(wgt_rows[LISTS * BLOCKS :, :], 0.0)
-        ident = held.tile([P, P], F32, name="ident")
-        make_identity(nc, ident[:])
-        turned = [psum.tile([P, P], F32, name="turned%d" % e) for e in range(2)]
+        turned = held.tile([P, 2, SQ], F32, name="turned", align_bytes=64)
         for e in range(2):
-            nc.tensor.transpose(turned[e][:], wgt_rows[:], ident[:])
-        wgt_parts = []
-        for j, width in enumerate(WGT_PARTS):
-            b0 = sum(WGT_PARTS[:j])
-            by_vector = j == 0
-            move = nc.vector.tensor_copy if by_vector else nc.scalar.copy
-            by_block = turned[0 if by_vector else 1][:, : LISTS * BLOCKS].rearrange("c (g b) -> c b g", b=BLOCKS)
-            wide = held.tile([P, width, LISTS, LIST_ROWS], F32, name="wide%d" % j)
-            move(wide[:], by_block[:, b0 : b0 + width, :].unsqueeze(3).to_broadcast([P, width, LISTS, LIST_ROWS]))
-            back = psum.tile([P, width, P], F32, name="back%d" % j)
-            for b in range(width):
-                nc.tensor.transpose(back[:, b, :], wide[:, b, :, :].rearrange("c g x -> c (g x)"), ident[:])
-            wgt_parts.append((b0 * P, (b0 + width) * P, move, back))
-        for lo, hi, move, back in wgt_parts:
-            move(wgt_sb[:, lo:hi], back[:].rearrange("p b c -> p (b c)"))
+            nc.vector.transpose(turned[:, e, :], wgt_rows[:, e * SQ : (e + 1) * SQ])
+        by_run = turned[:].rearrange("j e (h b) -> j b (e h)", h=2)
+        runs = LIST_ROWS // WGT_PARTS
+        wides = []
+        for j in range(WGT_PARTS):
+            wide = held.tile([P, runs, 4, LIST_ROWS], F32, name="wide%d" % j, align_bytes=64)
+            move = nc.vector.tensor_copy if j < WGT_PARTS // 2 else nc.scalar.copy
+            move(wide[:], by_run[:, j * runs : (j + 1) * runs, :].unsqueeze(3).to_broadcast([P, runs, 4, LIST_ROWS]))
+            wides.append(wide)
+        for j in range(WGT_PARTS):
+            part = PICKS // WGT_PARTS
+            nc.vector.transpose(wgt_sb[:, j * part : (j + 1) * part], wides[j][:].rearrange("j b y x -> j (b y x)"))
 
         last_pair = PLANES // 2 - 1
         short = PICKS - P
@@ -91,7 +85,8 @@ def tile_list_hbag_tm_res_kernel(tc, xT, w, wgt, r, offs, out):
             shift = short - PLANE6_CUT if lo < PLANE6_CUT else -PLANE6_CUT
             return slice(lo + shift, hi + shift)
 
-        x_at = [PASSES * M + a * PICKS for a in range(PASSES)]
+        w_at = [a * (M + PICKS) for a in range(PASSES)]
+        x_at = [w_at[a] + M for a in range(PASSES)]
         grouped_at = [0, x_at[1]]
         grouped = [held.tile([P, x_at[1], PACK], BF16, name="grouped0", align_bytes=64)]
         codes = held.tile([P, x_at[1] + PICKS], U32, name="codes", align_bytes=64)
@@ -117,7 +112,7 @@ def tile_list_hbag_tm_res_kernel(tc, xT, w, wgt, r, offs, out):
 
         def interleave_w(a):
             nc.scalar.copy(
-                grouped[0][:, a * M : (a + 1) * M, :].rearrange("p (n e) i -> p n i e", e=4),
+                grouped[0][:, w_at[a] : w_at[a] + M, :].rearrange("p (n e) i -> p n i e", e=4),
                 w_raw[:, a, :, :].rearrange("p i (n e) -> p n i e", e=4),
             )
 
@@ -135,21 +130,18 @@ def tile_list_hbag_tm_res_kernel(tc, xT, w, wgt, r, offs, out):
                     out=acc[b % HALVES][:],
                     lhsT=codes[:, c0 : c0 + P].bitcast(FP8X4),
                     lhsT_scale=scales[:, c0 : c0 + P],
-                    rhs=codes[:, a * M : (a + 1) * M].bitcast(FP8X4),
-                    rhs_scale=scales[:, a * M : (a + 1) * M],
+                    rhs=codes[:, w_at[a] : w_at[a] + M].bitcast(FP8X4),
+                    rhs_scale=scales[:, w_at[a] : w_at[a] + M],
                     start=(a == 0 and b // HALVES == 0),
                     stop=(a == PASSES - 1 and b // HALVES == G - 1),
                 )
 
-        quarter = PICKS - PICKS // 4
-        for lo, hi, move, back in wgt_parts:
-            gather(0, lo, hi)
+        gather(0, 0, PICKS)
         gather(1, 0, PICKS)
         interleave(0, 0, PICKS)
         gather(2, 0, PICKS)
         gather(3, 0, PICKS)
-        interleave(1, quarter, PICKS)
-        interleave(1, 0, quarter)
+        interleave(1, 0, PICKS)
 
         gather(4, 0, PICKS)
         gather(5, 0, PLANE5_CUT)
@@ -159,8 +151,8 @@ def tile_list_hbag_tm_res_kernel(tc, xT, w, wgt, r, offs, out):
         interleave(2, 0, PLANE5_CUT)
         gather(5, PLANE5_CUT, PICKS)
         interleave(2, PLANE5_CUT, PICKS)
-        quantize(0, x_at[0] + quarter, x_at[1])
-        quantize(0, 0, x_at[0] + quarter)
+        quantize(0, 0, PICKS)
+        quantize(0, PICKS, x_at[1])
         multiply(0, 0, PICKS)
 
         gather(6, 0, PLANE6_CUT)

@@ -28,7 +28,6 @@ SQ = 32
 WGT_PARTS = 4
 PLANES_BEFORE_W = 6
 PLANE5_CUT = 3 * P
-PLANE6_CUT = 5 * P
 
 
 def tile_list_hbag_tm_res_kernel(tc, xT, w, wgt, r, offs, out):
@@ -41,12 +40,43 @@ def tile_list_hbag_tm_res_kernel(tc, xT, w, wgt, r, offs, out):
         wgt_sb = held.tile([P, PICKS], F32, name="wgt_sb", align_bytes=64)
         wgt_rows = held.tile([P, 2 * SQ], F32, name="wgt_rows", align_bytes=64)
         planes = [held.tile([P, T], F32, name="plane%d" % q) for q in range(PLANES)]
-        w_raw = held.tile([P, PASSES, PACK, M], F32, name="w_raw", tag="w_then_pass1", align_bytes=64)
         r_sb = held.tile([P, HALVES, M], F32, name="r_sb")
         x_rows = xT.rearrange("(a p i) t -> a i p t", p=P, i=PACK)
 
         def load_plane(q):
             nc.sync.dma_start(planes[q][:], x_rows[q // PACK, q % PACK])
+
+        last_pair = PLANES // 2 - 1
+        picked = [held.tile([P, 2, PICKS], F32, name="picked%d" % u) for u in range(last_pair)]
+        parts = [(0, 64, 832), (256, 320, 896), (640, 704, 256), (896, 0, 128)]
+        staged = held.tile([P, 2112], F32, name="staged")
+
+        def products(u, lo, hi):
+            if u < last_pair:
+                return picked[u][:, :, lo:hi]
+            first, at, apart = [part for part in parts if part[0] <= lo][-1]
+            rows = staged[:, at : at + 2 * apart].rearrange("p (i m) -> p i m", i=2)
+            return rows[:, :, lo - first : hi - first]
+
+        last = PICKS - P
+        w_at = [PICKS, 0]
+        x_at = [M, PICKS + M]
+        spare_at = x_at[1] + PICKS
+        width = spare_at + P
+        grouped = held.tile([P, width * PACK], BF16, name="grouped", align_bytes=64)
+        codes = held.tile([P, width], U32, name="codes", align_bytes=64)
+        scales = held.tile([P, width], U8, name="scales", align_bytes=64)
+        raw_at = x_at[1] * PACK // 2
+        w_raw = grouped[:].bitcast(F32)[:, raw_at : raw_at + PASSES * PACK * M].rearrange("p (a i n) -> p a i n", a=PASSES, i=PACK)
+
+        def column_of(a, pick):
+            return spare_at + pick - last if a == 0 and pick >= last else x_at[a] + pick
+
+        def fours(lo, hi):
+            return grouped[:, lo * PACK : hi * PACK].rearrange("p (m i) -> p m i", i=PACK)
+
+        acc = [psum.tile([P, M], F32, name="acc%d" % h) for h in range(HALVES)]
+        result = [held.tile([P, M], F32, name="result%d" % h) for h in range(HALVES)]
 
         half_rows = wgt.rearrange("p (e b c) -> (p e) b c", e=2, c=2 * SQ)
         nc.sync.dma_start(wgt_rows[:], half_rows[:: LIST_ROWS + 1])
@@ -54,7 +84,7 @@ def tile_list_hbag_tm_res_kernel(tc, xT, w, wgt, r, offs, out):
         nc.sync.dma_start(offsets[:], offs)
         for q in range(1, PLANES_BEFORE_W):
             load_plane(q)
-        nc.sync.dma_start(w_raw[:], w.rearrange("(a p i) n -> p a i n", p=P, i=PACK))
+        nc.sync.dma_start(w_raw, w.rearrange("(a p i) n -> p a i n", p=P, i=PACK))
         for q in range(PLANES_BEFORE_W, PLANES):
             load_plane(q)
         nc.sync.dma_start(r_sb[:], r.rearrange("(h p) n -> p h n", p=P))
@@ -74,29 +104,9 @@ def tile_list_hbag_tm_res_kernel(tc, xT, w, wgt, r, offs, out):
             part = PICKS // WGT_PARTS
             nc.vector.transpose(wgt_sb[:, j * part : (j + 1) * part], wides[j][:].rearrange("j b y x -> j (b y x)"))
 
-        last_pair = PLANES // 2 - 1
-        short = PICKS - P
-        picked = [held.tile([P, 2, PICKS], F32, name="picked%d" % u) for u in range(last_pair)]
-        picked.append(held.tile([P, 2, short], F32, name="picked%d" % last_pair))
-
-        def columns_of(u, lo, hi):
-            if u < last_pair:
-                return slice(lo, hi)
-            shift = short - PLANE6_CUT if lo < PLANE6_CUT else -PLANE6_CUT
-            return slice(lo + shift, hi + shift)
-
-        w_at = [a * (M + PICKS) for a in range(PASSES)]
-        x_at = [w_at[a] + M for a in range(PASSES)]
-        grouped_at = [0, x_at[1]]
-        grouped = [held.tile([P, x_at[1], PACK], BF16, name="grouped0", align_bytes=64)]
-        codes = held.tile([P, x_at[1] + PICKS], U32, name="codes", align_bytes=64)
-        scales = held.tile([P, x_at[1] + PICKS], U8, name="scales", align_bytes=64)
-        acc = [psum.tile([P, M], F32, name="acc%d" % h) for h in range(HALVES)]
-        result = [held.tile([P, M], F32, name="result%d" % h) for h in range(HALVES)]
-
         def gather(q, lo, hi):
             nc.vector.tensor_tensor(
-                picked[q // 2][:, q % 2, columns_of(q // 2, lo, hi)],
+                products(q // 2, lo, hi)[:, q % 2, :],
                 planes[q][:].indirect(offsets[:, lo // LIST_ROWS : hi // LIST_ROWS]),
                 wgt_sb[:, lo:hi],
                 MULT,
@@ -104,74 +114,82 @@ def tile_list_hbag_tm_res_kernel(tc, xT, w, wgt, r, offs, out):
 
         def interleave(u, lo, hi):
             a, i0 = u // 2, 2 * (u % 2)
-            c0 = x_at[a] - grouped_at[a]
+            c0 = column_of(a, lo)
             nc.scalar.copy(
-                grouped[a][:, c0 + lo : c0 + hi, i0 : i0 + 2],
-                picked[u][:, :, columns_of(u, lo, hi)].rearrange("p i m -> p m i"),
+                fours(c0, c0 + hi - lo)[:, :, i0 : i0 + 2],
+                products(u, lo, hi).rearrange("p i m -> p m i"),
             )
 
         def interleave_w(a):
             nc.scalar.copy(
-                grouped[0][:, w_at[a] : w_at[a] + M, :].rearrange("p (n e) i -> p n i e", e=4),
+                fours(w_at[a], w_at[a] + M).rearrange("p (n e) i -> p n i e", e=4),
                 w_raw[:, a, :, :].rearrange("p i (n e) -> p n i e", e=4),
             )
 
-        def quantize(a, lo, hi):
+        def quantize(lo, hi):
             nc.vector.quantize_mx(
                 out=codes[:, lo:hi].bitcast(FP8X4),
                 scales=scales[:, lo:hi],
-                in_=grouped[a][:, lo - grouped_at[a] : hi - grouped_at[a], :].rearrange("p m i -> p (m i)"),
+                in_=grouped[:, lo * PACK : hi * PACK],
             )
 
-        def multiply(a, lo, hi):
-            for b in range(lo // P, hi // P):
-                c0 = x_at[a] + b * P
-                nc.tensor.matmul_mx(
-                    out=acc[b % HALVES][:],
-                    lhsT=codes[:, c0 : c0 + P].bitcast(FP8X4),
-                    lhsT_scale=scales[:, c0 : c0 + P],
-                    rhs=codes[:, w_at[a] : w_at[a] + M].bitcast(FP8X4),
-                    rhs_scale=scales[:, w_at[a] : w_at[a] + M],
-                    start=(a == 0 and b // HALVES == 0),
-                    stop=(a == PASSES - 1 and b // HALVES == G - 1),
-                )
+        def multiply(a, b, stop=False):
+            c0 = column_of(a, b * P)
+            nc.tensor.matmul_mx(
+                out=acc[b % HALVES][:],
+                lhsT=codes[:, c0 : c0 + P].bitcast(FP8X4),
+                lhsT_scale=scales[:, c0 : c0 + P],
+                rhs=codes[:, w_at[a] : w_at[a] + M].bitcast(FP8X4),
+                rhs_scale=scales[:, w_at[a] : w_at[a] + M],
+                start=(a == 0 and b < HALVES),
+                stop=stop,
+            )
 
-        gather(0, 0, PICKS)
-        gather(1, 0, PICKS)
-        interleave(0, 0, PICKS)
-        gather(2, 0, PICKS)
-        gather(3, 0, PICKS)
-        interleave(1, 0, PICKS)
-
+        for u in range(2):
+            gather(2 * u, 0, PICKS)
+            gather(2 * u + 1, 0, PICKS)
+            interleave(u, 0, last)
+            interleave(u, last, PICKS)
         gather(4, 0, PICKS)
-        gather(5, 0, PLANE5_CUT)
-        for a in range(PASSES):
+        gather(5, 0, PICKS)
+        for a in reversed(range(PASSES)):
             interleave_w(a)
-        grouped.append(held.tile([P, PICKS, PACK], BF16, name="grouped1", tag="w_then_pass1", align_bytes=64))
-        interleave(2, 0, PLANE5_CUT)
-        gather(5, PLANE5_CUT, PICKS)
-        interleave(2, PLANE5_CUT, PICKS)
-        quantize(0, 0, PICKS)
-        quantize(0, PICKS, x_at[1])
-        multiply(0, 0, PICKS)
+        interleave(2, 0, PICKS)
+        quantize(0, PICKS)
 
-        gather(6, 0, PLANE6_CUT)
-        gather(7, 0, 2 * P)
+        nc.vector.tensor_tensor(staged[:, 64:704], planes[6][:].indirect(offsets[:, 0:40]), wgt_sb[:, 0:640], MULT)
+        gather(7, 0, 256)
         interleave(last_pair, 0, P)
-        interleave(last_pair, P, 2 * P)
-        gather(7, 2 * P, PLANE6_CUT)
-        interleave(last_pair, 2 * P, PLANE6_CUT)
-        gather(6, PLANE6_CUT, PICKS)
-        gather(7, PLANE6_CUT, PLANE6_CUT + P)
-        interleave(last_pair, PLANE6_CUT, PLANE6_CUT + P)
-        gather(7, PLANE6_CUT + P, PICKS)
-        for lo in range(PLANE6_CUT + P, PICKS, P):
-            interleave(last_pair, lo, lo + P)
-        cuts = list(range(0, PICKS - P, 2 * P)) + [PICKS - P, PICKS]
-        for lo, hi in zip(cuts, cuts[1:]):
-            quantize(1, x_at[1] + lo, x_at[1] + hi)
-            multiply(1, lo, hi)
+        interleave(last_pair, P, 256)
+        gather(7, 256, 640)
+        interleave(last_pair, 256, 640)
+        gather(6, last, PICKS)
+        quantize(w_at[0], x_at[1] + P)
+        for b in range(BLOCKS - 1):
+            multiply(0, b)
+        multiply(1, 0)
+        gather(7, last, PICKS)
+        interleave(last_pair, last, PICKS)
+        gather(6, 640, last)
+        gather(7, 640, 768)
+        interleave(last_pair, 640, 768)
+        gather(7, 768, last)
+        interleave(last_pair, 768, 832)
+        interleave(last_pair, 832, last)
 
-        for h in range(HALVES):
+        for b in (1, 3):
+            quantize(x_at[1] + b * P, x_at[1] + (b + 2) * P)
+            multiply(1, b)
+            multiply(1, b + 1)
+        quantize(x_at[1] + last, width)
+        multiply(1, 7)
+        multiply(0, 7)
+        quantize(x_at[1] + 640, x_at[1] + 768)
+        multiply(1, 5, stop=True)
+        quantize(x_at[1] + 768, x_at[1] + 832)
+        quantize(x_at[1] + 832, x_at[1] + last)
+        multiply(1, 6, stop=True)
+
+        for h in reversed(range(HALVES)):
             nc.vector.tensor_tensor(result[h][:], acc[h][:], r_sb[:, h, :], ADD)
             nc.sync.dma_start(out[h * P : (h + 1) * P, :], result[h][:])

@@ -27,7 +27,7 @@ HALVES = S // P
 SQ = 32
 WGT_PARTS = 4
 PLANES_BEFORE_W = 6
-PLANE5_CUT = 3 * P
+LAST_PLANE_CUTS = (0, 2 * P, 5 * P, PICKS)
 
 
 def tile_list_hbag_tm_res_kernel(tc, xT, w, wgt, r, offs, out):
@@ -40,53 +40,51 @@ def tile_list_hbag_tm_res_kernel(tc, xT, w, wgt, r, offs, out):
         wgt_sb = held.tile([P, PICKS], F32, name="wgt_sb", align_bytes=64)
         wgt_rows = held.tile([P, 2 * SQ], F32, name="wgt_rows", align_bytes=64)
         planes = [held.tile([P, T], F32, name="plane%d" % q) for q in range(PLANES)]
+        picked = [held.tile([P, 2, PICKS], F32, name="picked%d" % u) for u in range(3)]
         r_sb = held.tile([P, HALVES, M], F32, name="r_sb")
-        x_rows = xT.rearrange("(a p i) t -> a i p t", p=P, i=PACK)
-
-        def load_plane(q):
-            nc.sync.dma_start(planes[q][:], x_rows[q // PACK, q % PACK])
-
-        last_pair = PLANES // 2 - 1
-        picked = [held.tile([P, 2, PICKS], F32, name="picked%d" % u) for u in range(last_pair)]
-        parts = [(0, 64, 832), (256, 320, 896), (640, 704, 256), (896, 0, 128)]
-        staged = held.tile([P, 2112], F32, name="staged")
-
-        def products(u, lo, hi):
-            if u < last_pair:
-                return picked[u][:, :, lo:hi]
-            first, at, apart = [part for part in parts if part[0] <= lo][-1]
-            rows = staged[:, at : at + 2 * apart].rearrange("p (i m) -> p i m", i=2)
-            return rows[:, :, lo - first : hi - first]
-
-        last = PICKS - P
-        w_at = [PICKS, 0]
-        x_at = [M, PICKS + M]
-        spare_at = x_at[1] + PICKS
-        width = spare_at + P
-        grouped = held.tile([P, width * PACK], BF16, name="grouped", align_bytes=64)
-        codes = held.tile([P, width], U32, name="codes", align_bytes=64)
-        scales = held.tile([P, width], U8, name="scales", align_bytes=64)
-        raw_at = x_at[1] * PACK // 2
-        w_raw = grouped[:].bitcast(F32)[:, raw_at : raw_at + PASSES * PACK * M].rearrange("p (a i n) -> p a i n", a=PASSES, i=PACK)
-
-        def column_of(a, pick):
-            return spare_at + pick - last if a == 0 and pick >= last else x_at[a] + pick
-
-        def fours(lo, hi):
-            return grouped[:, lo * PACK : hi * PACK].rearrange("p (m i) -> p m i", i=PACK)
-
         acc = [psum.tile([P, M], F32, name="acc%d" % h) for h in range(HALVES)]
         result = [held.tile([P, M], F32, name="result%d" % h) for h in range(HALVES)]
 
+        slot_of = [[1, 2, 5, 6, 7, 8, 9, 10], [4, 11, 12, 13, 14, 15, 16, 17]]
+        width = (2 * BLOCKS + PASSES) * P
+        grouped = held.tile([P, width * PACK], BF16, name="grouped", align_bytes=64)
+        codes = held.tile([P, width], U32, name="codes", align_bytes=64)
+        scales = held.tile([P, width], U8, name="scales", align_bytes=64)
+        fours = grouped[:].rearrange("p (m i) -> p m i", i=PACK)
+        w_at = [0, 3 * P]
+        raw_at = slot_of[1][2] * P * PACK // 2
+        w_raw = grouped[:].bitcast(F32)[:, raw_at : raw_at + PASSES * PACK * M].rearrange("p (a i n) -> p a i n", a=PASSES, i=PACK)
+        staged = held.tile([P, 2944], F32, name="staged")
+        runs7 = [(0, 1024), (768, 1088)]
+
+        def column_of(a, b):
+            return slot_of[a][b] * P
+
+        def column7(pick):
+            first, at = [run for run in runs7 if run[0] <= pick][-1]
+            return at + pick - first
+
+        def products(q, lo, hi):
+            if q < 6:
+                return picked[q // 2][:, q % 2, lo:hi]
+            at = column7(lo) if q == 7 else lo
+            return staged[:, at : at + hi - lo]
+
+        def pairs(u, lo, hi):
+            if u < 3:
+                return picked[u][:, :, lo:hi].rearrange("p i m -> p m i")
+            apart = column7(lo) - lo
+            return staged[:, lo : lo + 2 * apart].rearrange("p (i m) -> p m i", i=2)[:, : hi - lo, :]
+
+        x_rows = xT.rearrange("(a p i) t -> a i p t", p=P, i=PACK)
         half_rows = wgt.rearrange("p (e b c) -> (p e) b c", e=2, c=2 * SQ)
         nc.sync.dma_start(wgt_rows[:], half_rows[:: LIST_ROWS + 1])
-        load_plane(0)
-        nc.sync.dma_start(offsets[:], offs)
-        for q in range(1, PLANES_BEFORE_W):
-            load_plane(q)
-        nc.sync.dma_start(w_raw, w.rearrange("(a p i) n -> p a i n", p=P, i=PACK))
-        for q in range(PLANES_BEFORE_W, PLANES):
-            load_plane(q)
+        for q in range(PLANES):
+            if q == PLANES_BEFORE_W:
+                nc.sync.dma_start(w_raw, w.rearrange("(a p i) n -> p a i n", p=P, i=PACK))
+            nc.sync.dma_start(planes[q][:], x_rows[q // PACK, q % PACK])
+            if q == 0:
+                nc.sync.dma_start(offsets[:], offs)
         nc.sync.dma_start(r_sb[:], r.rearrange("(h p) n -> p h n", p=P))
 
         turned = held.tile([P, 2, SQ], F32, name="turned", align_bytes=64)
@@ -106,7 +104,7 @@ def tile_list_hbag_tm_res_kernel(tc, xT, w, wgt, r, offs, out):
 
         def gather(q, lo, hi):
             nc.vector.tensor_tensor(
-                products(q // 2, lo, hi)[:, q % 2, :],
+                products(q, lo, hi),
                 planes[q][:].indirect(offsets[:, lo // LIST_ROWS : hi // LIST_ROWS]),
                 wgt_sb[:, lo:hi],
                 MULT,
@@ -114,15 +112,12 @@ def tile_list_hbag_tm_res_kernel(tc, xT, w, wgt, r, offs, out):
 
         def interleave(u, lo, hi):
             a, i0 = u // 2, 2 * (u % 2)
-            c0 = column_of(a, lo)
-            nc.scalar.copy(
-                fours(c0, c0 + hi - lo)[:, :, i0 : i0 + 2],
-                products(u, lo, hi).rearrange("p i m -> p m i"),
-            )
+            c0 = column_of(a, lo // P) + lo % P
+            nc.scalar.copy(fours[:, c0 : c0 + hi - lo, i0 : i0 + 2], pairs(u, lo, hi))
 
         def interleave_w(a):
             nc.scalar.copy(
-                fours(w_at[a], w_at[a] + M).rearrange("p (n e) i -> p n i e", e=4),
+                fours[:, w_at[a] : w_at[a] + M, :].rearrange("p (n e) i -> p n i e", e=4),
                 w_raw[:, a, :, :].rearrange("p i (n e) -> p n i e", e=4),
             )
 
@@ -133,8 +128,8 @@ def tile_list_hbag_tm_res_kernel(tc, xT, w, wgt, r, offs, out):
                 in_=grouped[:, lo * PACK : hi * PACK],
             )
 
-        def multiply(a, b, stop=False):
-            c0 = column_of(a, b * P)
+        def multiply(a, b):
+            c0 = column_of(a, b)
             nc.tensor.matmul_mx(
                 out=acc[b % HALVES][:],
                 lhsT=codes[:, c0 : c0 + P].bitcast(FP8X4),
@@ -142,54 +137,46 @@ def tile_list_hbag_tm_res_kernel(tc, xT, w, wgt, r, offs, out):
                 rhs=codes[:, w_at[a] : w_at[a] + M].bitcast(FP8X4),
                 rhs_scale=scales[:, w_at[a] : w_at[a] + M],
                 start=(a == 0 and b < HALVES),
-                stop=stop,
+                stop=(a == 1 and b >= BLOCKS - HALVES),
             )
 
         for u in range(2):
             gather(2 * u, 0, PICKS)
             gather(2 * u + 1, 0, PICKS)
-            interleave(u, 0, last)
-            interleave(u, last, PICKS)
+            for lo, hi in ((0, 256), (256, PICKS)):
+                interleave(u, lo, hi)
         gather(4, 0, PICKS)
         gather(5, 0, PICKS)
-        for a in reversed(range(PASSES)):
+        for a in range(PASSES):
             interleave_w(a)
-        interleave(2, 0, PICKS)
-        quantize(0, PICKS)
-
-        nc.vector.tensor_tensor(staged[:, 64:704], planes[6][:].indirect(offsets[:, 0:40]), wgt_sb[:, 0:640], MULT)
-        gather(7, 0, 256)
-        interleave(last_pair, 0, P)
-        interleave(last_pair, P, 256)
-        gather(7, 256, 640)
-        interleave(last_pair, 256, 640)
-        gather(6, last, PICKS)
-        quantize(w_at[0], x_at[1] + P)
-        for b in range(BLOCKS - 1):
+        for lo, hi in ((P, PICKS), (0, P)):
+            interleave(2, lo, hi)
+        for b in range(2):
+            quantize(2 * b * P, 2 * (b + 1) * P)
             multiply(0, b)
-        multiply(1, 0)
-        gather(7, last, PICKS)
-        interleave(last_pair, last, PICKS)
-        gather(6, 640, last)
-        gather(7, 640, 768)
-        interleave(last_pair, 640, 768)
-        gather(7, 768, last)
-        interleave(last_pair, 768, 832)
-        interleave(last_pair, 832, last)
-
-        for b in (1, 3):
-            quantize(x_at[1] + b * P, x_at[1] + (b + 2) * P)
+        gather(6, 0, PICKS)
+        gather(7, 0, 320)
+        interleave(3, 0, P)
+        interleave(3, P, 320)
+        gather(7, 320, 768)
+        interleave(3, 320, 768)
+        for b in range(2):
+            quantize(4 * (b + 1) * P, 4 * (b + 2) * P)
+            for c in range(3):
+                multiply(0, 2 + 3 * b + c)
             multiply(1, b)
-            multiply(1, b + 1)
-        quantize(x_at[1] + last, width)
+        gather(7, 768, 896)
+        interleave(3, 768, 896)
+        gather(7, 896, PICKS)
+        interleave(3, 896, 960)
+        interleave(3, 960, PICKS)
+        for b in range(2, BLOCKS - 1):
+            quantize(column_of(1, b), column_of(1, b) + P)
+            multiply(1, b)
+        quantize(column_of(1, 7), column_of(1, 7) + P // 2)
+        quantize(column_of(1, 7) + P // 2, column_of(1, 7) + P)
         multiply(1, 7)
-        multiply(0, 7)
-        quantize(x_at[1] + 640, x_at[1] + 768)
-        multiply(1, 5, stop=True)
-        quantize(x_at[1] + 768, x_at[1] + 832)
-        quantize(x_at[1] + 832, x_at[1] + last)
-        multiply(1, 6, stop=True)
 
-        for h in reversed(range(HALVES)):
+        for h in range(HALVES):
             nc.vector.tensor_tensor(result[h][:], acc[h][:], r_sb[:, h, :], ADD)
             nc.sync.dma_start(out[h * P : (h + 1) * P, :], result[h][:])

@@ -55,7 +55,7 @@ def tile_list_hbag_tm_res_kernel(tc, xT, w, wgt, r, offs, out):
         raw_at = slot_of[1][2] * P * PACK // 2
         w_raw = grouped[:].bitcast(F32)[:, raw_at : raw_at + PASSES * PACK * M].rearrange("p (a i n) -> p a i n", a=PASSES, i=PACK)
         staged = held.tile([P, 2944], F32, name="staged")
-        runs7 = [(0, 1024), (768, 1088)]
+        runs7 = [(0, 1152), (640, 1024), (896, 1280)]
 
         def column_of(a, b):
             return slot_of[a][b] * P
@@ -95,8 +95,7 @@ def tile_list_hbag_tm_res_kernel(tc, xT, w, wgt, r, offs, out):
         wides = []
         for j in range(WGT_PARTS):
             wide = held.tile([P, runs, 4, LIST_ROWS], F32, name="wide%d" % j, align_bytes=64)
-            move = nc.vector.tensor_copy if j < WGT_PARTS // 2 else nc.scalar.copy
-            move(wide[:], by_run[:, j * runs : (j + 1) * runs, :].unsqueeze(3).to_broadcast([P, runs, 4, LIST_ROWS]))
+            nc.vector.tensor_copy(wide[:], by_run[:, j * runs : (j + 1) * runs, :].unsqueeze(3).to_broadcast([P, runs, 4, LIST_ROWS]))
             wides.append(wide)
         for j in range(WGT_PARTS):
             part = PICKS // WGT_PARTS
@@ -155,18 +154,21 @@ def tile_list_hbag_tm_res_kernel(tc, xT, w, wgt, r, offs, out):
             quantize(2 * b * P, 2 * (b + 1) * P)
             multiply(0, b)
         gather(6, 0, PICKS)
-        gather(7, 0, 320)
-        interleave(3, 0, P)
-        interleave(3, P, 320)
-        gather(7, 320, 768)
-        interleave(3, 320, 768)
-        for b in range(2):
+        def late_call(b):
             quantize(4 * (b + 1) * P, 4 * (b + 2) * P)
             for c in range(3):
                 multiply(0, 2 + 3 * b + c)
             multiply(1, b)
-        gather(7, 768, 896)
-        interleave(3, 768, 896)
+
+        gather(7, 0, 256)
+        interleave(3, 0, P)
+        interleave(3, P, 256)
+        gather(7, 256, 640)
+        interleave(3, 256, 640)
+        late_call(0)
+        gather(7, 640, 896)
+        interleave(3, 640, 896)
+        late_call(1)
         gather(7, 896, PICKS)
         interleave(3, 896, 960)
         interleave(3, 960, PICKS)

@@ -27,7 +27,8 @@ HALVES = S // P
 SQ = 32
 WGT_PARTS = 4
 PLANES_BEFORE_W = 6
-LAST_PLANE_CUTS = (0, 2 * P, 5 * P, PICKS)
+EARLY_RUNS = 3
+CUT_A, CUT_B = 2 * P, 5 * P
 
 
 def tile_list_hbag_tm_res_kernel(tc, xT, w, wgt, r, offs, out):
@@ -45,24 +46,25 @@ def tile_list_hbag_tm_res_kernel(tc, xT, w, wgt, r, offs, out):
         acc = [psum.tile([P, M], F32, name="acc%d" % h) for h in range(HALVES)]
         result = [held.tile([P, M], F32, name="result%d" % h) for h in range(HALVES)]
 
-        slot_of = [[1, 2, 5, 6, 7, 8, 9, 10], [4, 11, 12, 13, 14, 15, 16, 17]]
-        width = (2 * BLOCKS + PASSES) * P
-        grouped = held.tile([P, width * PACK], BF16, name="grouped", align_bytes=64)
-        codes = held.tile([P, width], U32, name="codes", align_bytes=64)
-        scales = held.tile([P, width], U8, name="scales", align_bytes=64)
-        fours = grouped[:].rearrange("p (m i) -> p m i", i=PACK)
-        w_at = [0, 3 * P]
-        raw_at = slot_of[1][2] * P * PACK // 2
+        grouped = held.tile([P, 18 * P * PACK], BF16, name="grouped", align_bytes=64)
+        codes = held.tile([P, 13 * P], U32, name="codes", align_bytes=64)
+        scales = held.tile([P, 13 * P], U8, name="scales", align_bytes=64)
+        w_slot = [4, 0]
+        raw_at = 9 * P * PACK // 2
         w_raw = grouped[:].bitcast(F32)[:, raw_at : raw_at + PASSES * PACK * M].rearrange("p (a i n) -> p a i n", a=PASSES, i=PACK)
-        staged = held.tile([P, 2944], F32, name="staged")
-        runs7 = [(0, 1152), (640, 1024), (896, 1280)]
+        fours = grouped[:].rearrange("p (m i) -> p m i", i=PACK)
+        code_slot = [[1, 2, 3, 1, 2, 3, 5, 1], [5, 6, 7, 8, 9, 10, 11, 12]]
 
-        def column_of(a, b):
-            return slot_of[a][b] * P
+        def slot_of(a, b):
+            if a == 1:
+                return 5 + b
+            return 1 + b if b < EARLY_RUNS else 10 + b
+
+        first_at = PICKS + (PICKS - CUT_B) - P
+        staged = held.tile([P, 2 * first_at + CUT_B], F32, name="staged")
 
         def column7(pick):
-            first, at = [run for run in runs7 if run[0] <= pick][-1]
-            return at + pick - first
+            return first_at + pick if pick < CUT_B else PICKS + pick - CUT_B
 
         def products(q, lo, hi):
             if q < 6:
@@ -111,30 +113,35 @@ def tile_list_hbag_tm_res_kernel(tc, xT, w, wgt, r, offs, out):
 
         def interleave(u, lo, hi):
             a, i0 = u // 2, 2 * (u % 2)
-            c0 = column_of(a, lo // P) + lo % P
+            c0 = slot_of(a, lo // P) * P + lo % P
             nc.scalar.copy(fours[:, c0 : c0 + hi - lo, i0 : i0 + 2], pairs(u, lo, hi))
 
         def interleave_w(a):
+            at = w_slot[a] * P
             nc.scalar.copy(
-                fours[:, w_at[a] : w_at[a] + M, :].rearrange("p (n e) i -> p n i e", e=4),
+                fours[:, at : at + M, :].rearrange("p (n e) i -> p n i e", e=4),
                 w_raw[:, a, :, :].rearrange("p i (n e) -> p n i e", e=4),
             )
 
-        def quantize(lo, hi):
+        def quantize(lo, hi, to):
             nc.vector.quantize_mx(
-                out=codes[:, lo:hi].bitcast(FP8X4),
-                scales=scales[:, lo:hi],
+                out=codes[:, to : to + hi - lo].bitcast(FP8X4),
+                scales=scales[:, to : to + hi - lo],
                 in_=grouped[:, lo * PACK : hi * PACK],
             )
 
+        def one_run(a, b):
+            quantize(slot_of(a, b) * P, (slot_of(a, b) + 1) * P, code_slot[a][b] * P)
+            multiply(a, b)
+
         def multiply(a, b):
-            c0 = column_of(a, b)
+            c0, w0 = code_slot[a][b] * P, w_slot[a] * P
             nc.tensor.matmul_mx(
                 out=acc[b % HALVES][:],
                 lhsT=codes[:, c0 : c0 + P].bitcast(FP8X4),
                 lhsT_scale=scales[:, c0 : c0 + P],
-                rhs=codes[:, w_at[a] : w_at[a] + M].bitcast(FP8X4),
-                rhs_scale=scales[:, w_at[a] : w_at[a] + M],
+                rhs=codes[:, w0 : w0 + M].bitcast(FP8X4),
+                rhs_scale=scales[:, w0 : w0 + M],
                 start=(a == 0 and b < HALVES),
                 stop=(a == 1 and b >= BLOCKS - HALVES),
             )
@@ -142,41 +149,33 @@ def tile_list_hbag_tm_res_kernel(tc, xT, w, wgt, r, offs, out):
         for u in range(2):
             gather(2 * u, 0, PICKS)
             gather(2 * u + 1, 0, PICKS)
-            for lo, hi in ((0, 256), (256, PICKS)):
-                interleave(u, lo, hi)
+            interleave(u, 0, EARLY_RUNS * P)
+            interleave(u, EARLY_RUNS * P, PICKS)
         gather(4, 0, PICKS)
         gather(5, 0, PICKS)
-        for a in range(PASSES):
-            interleave_w(a)
-        for lo, hi in ((P, PICKS), (0, P)):
-            interleave(2, lo, hi)
-        for b in range(2):
-            quantize(2 * b * P, 2 * (b + 1) * P)
-            multiply(0, b)
+        interleave_w(1)
+        interleave_w(0)
+        interleave(2, 0, PICKS)
+        quantize(0, 4 * P, 0)
         gather(6, 0, PICKS)
-        def late_call(b):
-            quantize(4 * (b + 1) * P, 4 * (b + 2) * P)
-            for c in range(3):
-                multiply(0, 2 + 3 * b + c)
-            multiply(1, b)
 
-        gather(7, 0, 256)
+        gather(7, 0, CUT_A)
         interleave(3, 0, P)
-        interleave(3, P, 256)
-        gather(7, 256, 640)
-        interleave(3, 256, 640)
-        late_call(0)
-        gather(7, 640, 896)
-        interleave(3, 640, 896)
-        late_call(1)
-        gather(7, 896, PICKS)
-        interleave(3, 896, 960)
-        interleave(3, 960, PICKS)
-        for b in range(2, BLOCKS - 1):
-            quantize(column_of(1, b), column_of(1, b) + P)
-            multiply(1, b)
-        quantize(column_of(1, 7), column_of(1, 7) + P // 2)
-        quantize(column_of(1, 7) + P // 2, column_of(1, 7) + P)
+        interleave(3, P, CUT_A)
+        gather(7, CUT_A, CUT_B)
+        interleave(3, CUT_A, CUT_B)
+        quantize(4 * P, 6 * P, 4 * P)
+        for b in range(EARLY_RUNS):
+            multiply(0, b)
+        multiply(1, 0)
+        gather(7, CUT_B, PICKS)
+        for lo, hi in ((CUT_B, 6 * P), (6 * P, 7 * P), (7 * P, 7 * P + P // 2), (7 * P + P // 2, PICKS)):
+            interleave(3, lo, hi)
+        for a, b in ((0, 3), (0, 4), (0, 5), (0, 6), (1, 1), (1, 2), (0, 7), (1, 3), (1, 4), (1, 5), (1, 6)):
+            one_run(a, b)
+        last = slot_of(1, 7) * P
+        quantize(last, last + P // 2, last)
+        quantize(last + P // 2, last + P, last + P // 2)
         multiply(1, 7)
 
         for h in range(HALVES):

@@ -27,8 +27,7 @@ HALVES = S // P
 SQ = 32
 WGT_PARTS = 4
 PLANES_BEFORE_W = 6
-EARLY_RUNS = 3
-CUT_A, CUT_B = 2 * P, 5 * P
+CUT_A, CUT_B = 320, 768
 
 
 def tile_list_hbag_tm_res_kernel(tc, xT, w, wgt, r, offs, out):
@@ -46,22 +45,19 @@ def tile_list_hbag_tm_res_kernel(tc, xT, w, wgt, r, offs, out):
         acc = [psum.tile([P, M], F32, name="acc%d" % h) for h in range(HALVES)]
         result = [held.tile([P, M], F32, name="result%d" % h) for h in range(HALVES)]
 
-        grouped = held.tile([P, 18 * P * PACK], BF16, name="grouped", align_bytes=64)
-        codes = held.tile([P, 13 * P], U32, name="codes", align_bytes=64)
-        scales = held.tile([P, 13 * P], U8, name="scales", align_bytes=64)
-        w_slot = [4, 0]
-        raw_at = 9 * P * PACK // 2
-        w_raw = grouped[:].bitcast(F32)[:, raw_at : raw_at + PASSES * PACK * M].rearrange("p (a i n) -> p a i n", a=PASSES, i=PACK)
+        width = (2 * BLOCKS + PASSES) * P
+        grouped = held.tile([P, width * PACK], BF16, name="grouped", align_bytes=64)
+        codes = held.tile([P, width], U32, name="codes", align_bytes=64)
+        scales = held.tile([P, width], U8, name="scales", align_bytes=64)
         fours = grouped[:].rearrange("p (m i) -> p m i", i=PACK)
-        code_slot = [[1, 2, 3, 1, 2, 3, 5, 1], [5, 6, 7, 8, 9, 10, 11, 12]]
-
-        def slot_of(a, b):
-            if a == 1:
-                return 5 + b
-            return 1 + b if b < EARLY_RUNS else 10 + b
-
+        w_at = [0, (2 * BLOCKS + 1) * P]
+        raw_at = 12 * P * PACK // 2
+        w_raw = grouped[:].bitcast(F32)[:, raw_at : raw_at + PASSES * PACK * M].rearrange("p (a i n) -> p a i n", a=PASSES, i=PACK)
         first_at = PICKS + (PICKS - CUT_B) - P
         staged = held.tile([P, 2 * first_at + CUT_B], F32, name="staged")
+
+        def column_of(a, b):
+            return (1 + BLOCKS * a + b) * P
 
         def column7(pick):
             return first_at + pick if pick < CUT_B else PICKS + pick - CUT_B
@@ -113,69 +109,69 @@ def tile_list_hbag_tm_res_kernel(tc, xT, w, wgt, r, offs, out):
 
         def interleave(u, lo, hi):
             a, i0 = u // 2, 2 * (u % 2)
-            c0 = slot_of(a, lo // P) * P + lo % P
+            c0 = column_of(a, lo // P) + lo % P
             nc.scalar.copy(fours[:, c0 : c0 + hi - lo, i0 : i0 + 2], pairs(u, lo, hi))
 
         def interleave_w(a):
-            at = w_slot[a] * P
             nc.scalar.copy(
-                fours[:, at : at + M, :].rearrange("p (n e) i -> p n i e", e=4),
+                fours[:, w_at[a] : w_at[a] + M, :].rearrange("p (n e) i -> p n i e", e=4),
                 w_raw[:, a, :, :].rearrange("p i (n e) -> p n i e", e=4),
             )
 
-        def quantize(lo, hi, to):
+        def quantize(lo, hi, to=None):
+            to = lo if to is None else to
             nc.vector.quantize_mx(
                 out=codes[:, to : to + hi - lo].bitcast(FP8X4),
                 scales=scales[:, to : to + hi - lo],
                 in_=grouped[:, lo * PACK : hi * PACK],
             )
 
-        def one_run(a, b):
-            quantize(slot_of(a, b) * P, (slot_of(a, b) + 1) * P, code_slot[a][b] * P)
-            multiply(a, b)
+        def codes_of(a, b):
+            return column_of(0, b + 4) if a == 0 and 1 <= b <= 4 else column_of(a, b)
 
         def multiply(a, b):
-            c0, w0 = code_slot[a][b] * P, w_slot[a] * P
+            c0 = codes_of(a, b)
             nc.tensor.matmul_mx(
                 out=acc[b % HALVES][:],
                 lhsT=codes[:, c0 : c0 + P].bitcast(FP8X4),
                 lhsT_scale=scales[:, c0 : c0 + P],
-                rhs=codes[:, w0 : w0 + M].bitcast(FP8X4),
-                rhs_scale=scales[:, w0 : w0 + M],
-                start=(a == 0 and b < HALVES),
+                rhs=codes[:, w_at[a] : w_at[a] + M].bitcast(FP8X4),
+                rhs_scale=scales[:, w_at[a] : w_at[a] + M],
+                start=(a, b) in ((0, 0), (0, 5)),
                 stop=(a == 1 and b >= BLOCKS - HALVES),
             )
 
         for u in range(2):
             gather(2 * u, 0, PICKS)
             gather(2 * u + 1, 0, PICKS)
-            interleave(u, 0, EARLY_RUNS * P)
-            interleave(u, EARLY_RUNS * P, PICKS)
+            interleave(u, 0, PICKS)
         gather(4, 0, PICKS)
         gather(5, 0, PICKS)
-        interleave_w(1)
-        interleave_w(0)
+        for a in range(PASSES):
+            interleave_w(a)
         interleave(2, 0, PICKS)
-        quantize(0, 4 * P, 0)
+        quantize(0, 2 * P)
+        multiply(0, 0)
+        quantize(w_at[1], w_at[1] + M)
         gather(6, 0, PICKS)
 
         gather(7, 0, CUT_A)
         interleave(3, 0, P)
         interleave(3, P, CUT_A)
         gather(7, CUT_A, CUT_B)
-        interleave(3, CUT_A, CUT_B)
-        quantize(4 * P, 6 * P, 4 * P)
-        for b in range(EARLY_RUNS):
-            multiply(0, b)
-        multiply(1, 0)
+        interleave(3, CUT_A, 3 * P)
+        interleave(3, 3 * P, CUT_B)
+        quantize(column_of(0, 5), column_of(1, 1))
+        for a, b in ((0, 5), (0, 6), (0, 7), (1, 0)):
+            multiply(a, b)
         gather(7, CUT_B, PICKS)
-        for lo, hi in ((CUT_B, 6 * P), (6 * P, 7 * P), (7 * P, 7 * P + P // 2), (7 * P + P // 2, PICKS)):
+        for lo, hi in ((CUT_B, 7 * P), (7 * P, 7 * P + P // 2), (7 * P + P // 2, PICKS)):
             interleave(3, lo, hi)
-        for a, b in ((0, 3), (0, 4), (0, 5), (0, 6), (1, 1), (1, 2), (0, 7), (1, 3), (1, 4), (1, 5), (1, 6)):
-            one_run(a, b)
-        last = slot_of(1, 7) * P
-        quantize(last, last + P // 2, last)
-        quantize(last + P // 2, last + P, last + P // 2)
+        for a, b in ((1, 1), (1, 2), (0, 1), (0, 2), (0, 3), (0, 4), (1, 3), (1, 4), (1, 6), (1, 5)):
+            quantize(column_of(a, b), column_of(a, b) + P, codes_of(a, b))
+            multiply(a, b)
+        quantize(column_of(1, 7), column_of(1, 7) + P // 2)
+        quantize(column_of(1, 7) + P // 2, column_of(1, 7) + P)
         multiply(1, 7)
 
         for h in range(HALVES):

@@ -50,14 +50,14 @@ def tile_list_hbag_tm_res_kernel(tc, xT, w, wgt, r, offs, out):
         codes = held.tile([P, width], U32, name="codes", align_bytes=64)
         scales = held.tile([P, width], U8, name="scales", align_bytes=64)
         fours = grouped[:].rearrange("p (m i) -> p m i", i=PACK)
-        w_at = [0, (2 * BLOCKS + 1) * P]
+        w_at = [0, (BLOCKS + 1) * P]
         raw_at = 12 * P * PACK // 2
         w_raw = grouped[:].bitcast(F32)[:, raw_at : raw_at + PASSES * PACK * M].rearrange("p (a i n) -> p a i n", a=PASSES, i=PACK)
         first_at = PICKS + (PICKS - CUT_B) - P
         staged = held.tile([P, 2 * first_at + CUT_B], F32, name="staged")
 
         def column_of(a, b):
-            return (1 + BLOCKS * a + b) * P
+            return (1 + (BLOCKS + 1) * a + b) * P
 
         def column7(pick):
             return first_at + pick if pick < CUT_B else PICKS + pick - CUT_B
@@ -127,7 +127,8 @@ def tile_list_hbag_tm_res_kernel(tc, xT, w, wgt, r, offs, out):
             )
 
         def codes_of(a, b):
-            return column_of(0, b + 4) if a == 0 and 1 <= b <= 4 else column_of(a, b)
+            spent = [(0, 6), (0, 7), (1, 0), (1, 1), (1, 2)]
+            return column_of(*spent[b - 1]) if a == 0 and 1 <= b <= 5 else column_of(a, b)
 
         def multiply(a, b):
             c0 = codes_of(a, b)
@@ -137,7 +138,7 @@ def tile_list_hbag_tm_res_kernel(tc, xT, w, wgt, r, offs, out):
                 lhsT_scale=scales[:, c0 : c0 + P],
                 rhs=codes[:, w_at[a] : w_at[a] + M].bitcast(FP8X4),
                 rhs_scale=scales[:, w_at[a] : w_at[a] + M],
-                start=(a, b) in ((0, 0), (0, 5)),
+                start=(a, b) in ((0, 0), (0, 7)),
                 stop=(a == 1 and b >= BLOCKS - HALVES),
             )
 
@@ -152,7 +153,6 @@ def tile_list_hbag_tm_res_kernel(tc, xT, w, wgt, r, offs, out):
         interleave(2, 0, PICKS)
         quantize(0, 2 * P)
         multiply(0, 0)
-        quantize(w_at[1], w_at[1] + M)
         gather(6, 0, PICKS)
 
         gather(7, 0, CUT_A)
@@ -161,13 +161,13 @@ def tile_list_hbag_tm_res_kernel(tc, xT, w, wgt, r, offs, out):
         gather(7, CUT_A, CUT_B)
         interleave(3, CUT_A, 3 * P)
         interleave(3, 3 * P, CUT_B)
-        quantize(column_of(0, 5), column_of(1, 1))
-        for a, b in ((0, 5), (0, 6), (0, 7), (1, 0)):
+        quantize(column_of(0, 6), column_of(1, 1))
+        for a, b in ((0, 6), (0, 7), (1, 0)):
             multiply(a, b)
         gather(7, CUT_B, PICKS)
         for lo, hi in ((CUT_B, 7 * P), (7 * P, 7 * P + P // 2), (7 * P + P // 2, PICKS)):
             interleave(3, lo, hi)
-        for a, b in ((1, 1), (1, 2), (0, 1), (0, 2), (0, 3), (0, 4), (1, 3), (1, 4), (1, 6), (1, 5)):
+        for a, b in ((1, 1), (1, 2), (0, 1), (0, 2), (0, 3), (1, 3), (0, 4), (0, 5), (1, 4), (1, 6), (1, 5)):
             quantize(column_of(a, b), column_of(a, b) + P, codes_of(a, b))
             multiply(a, b)
         quantize(column_of(1, 7), column_of(1, 7) + P // 2)

@@ -127,7 +127,7 @@ def tile_list_hbag_tm_res_kernel(tc, xT, w, wgt, r, offs, out):
             )
 
         def codes_of(a, b):
-            spent = [(0, 6), (0, 7), (1, 0), (1, 1), (1, 2)]
+            spent = [(0, 6), (0, 7), (1, 0), (0, 0), (1, 1)]
             return column_of(*spent[b - 1]) if a == 0 and 1 <= b <= 5 else column_of(a, b)
 
         def multiply(a, b):
@@ -138,7 +138,7 @@ def tile_list_hbag_tm_res_kernel(tc, xT, w, wgt, r, offs, out):
                 lhsT_scale=scales[:, c0 : c0 + P],
                 rhs=codes[:, w_at[a] : w_at[a] + M].bitcast(FP8X4),
                 rhs_scale=scales[:, w_at[a] : w_at[a] + M],
-                start=(a, b) in ((0, 0), (0, 7)),
+                start=(a, b) in ((0, 6), (0, 7)),
                 stop=(a == 1 and b >= BLOCKS - HALVES),
             )
 
@@ -152,22 +152,21 @@ def tile_list_hbag_tm_res_kernel(tc, xT, w, wgt, r, offs, out):
             interleave_w(a)
         interleave(2, 0, PICKS)
         quantize(0, 2 * P)
-        multiply(0, 0)
         gather(6, 0, PICKS)
 
         gather(7, 0, CUT_A)
         interleave(3, 0, P)
         interleave(3, P, CUT_A)
         gather(7, CUT_A, CUT_B)
-        interleave(3, CUT_A, 3 * P)
-        interleave(3, 3 * P, CUT_B)
+        interleave(3, CUT_A, 4 * P)
+        interleave(3, 4 * P, CUT_B)
         quantize(column_of(0, 6), column_of(1, 1))
-        for a, b in ((0, 6), (0, 7), (1, 0)):
+        for a, b in ((0, 6), (0, 7), (1, 0), (0, 0)):
             multiply(a, b)
         gather(7, CUT_B, PICKS)
         for lo, hi in ((CUT_B, 7 * P), (7 * P, 7 * P + P // 2), (7 * P + P // 2, PICKS)):
             interleave(3, lo, hi)
-        for a, b in ((1, 1), (1, 2), (0, 1), (0, 2), (0, 3), (1, 3), (0, 4), (0, 5), (1, 4), (1, 6), (1, 5)):
+        for a, b in ((1, 1), (1, 2), (1, 3), (0, 1), (0, 2), (0, 3), (0, 4), (1, 4), (1, 5), (1, 6), (0, 5)):
             quantize(column_of(a, b), column_of(a, b) + P, codes_of(a, b))
             multiply(a, b)
         quantize(column_of(1, 7), column_of(1, 7) + P // 2)

@@ -27,34 +27,37 @@ HALVES = S // P
 SQ = 32
 WGT_PARTS = 4
 PLANES_BEFORE_W = 6
+KIB = 1024
+EVEN_AT, STAGE_AT, ODD_AT, MX_AT = 0, 64 * KIB, 128 * KIB, 192 * KIB
 CUT_A, CUT_B = 320, 768
 
 
 def tile_list_hbag_tm_res_kernel(tc, xT, w, wgt, r, offs, out):
     nc = tc.nc
     with ExitStack() as ctx:
+        lists = ctx.enter_context(tc.tile_pool(name="lists", bufs=1))
         held = ctx.enter_context(tc.tile_pool(name="held", bufs=1))
         psum = ctx.enter_context(tc.psum_pool(name="psum", bufs=1))
 
-        offsets = held.tile([P, PICKS // LIST_ROWS], U16, name="offsets")
-        wgt_sb = held.tile([P, PICKS], F32, name="wgt_sb", align_bytes=64)
-        wgt_rows = held.tile([P, 2 * SQ], F32, name="wgt_rows", align_bytes=64)
-        planes = [held.tile([P, T], F32, name="plane%d" % q) for q in range(PLANES)]
-        picked = [held.tile([P, 2, PICKS], F32, name="picked%d" % u) for u in range(3)]
-        r_sb = held.tile([P, HALVES, M], F32, name="r_sb")
+        offsets = lists.tile([P, PICKS // LIST_ROWS], U16, name="offsets")
+        wgt_sb = held.tile([P, PICKS], F32, name="wgt_sb", align_bytes=64, offset=STAGE_AT)
+        wgt_rows = held.tile([P, 2 * SQ], F32, name="wgt_rows", align_bytes=64, offset=STAGE_AT + 4 * KIB)
+        planes = [held.tile([P, T], F32, name="plane%d" % q, offset=(ODD_AT if q % 2 else EVEN_AT) + q // 2 * 8 * KIB) for q in range(PLANES)]
+        picked = [held.tile([P, 2, PICKS], F32, name="picked%d" % u, offset=STAGE_AT + (20 + 8 * u) * KIB) for u in range(3)]
+        r_sb = held.tile([P, HALVES, M], F32, name="r_sb", offset=MX_AT + 30 * KIB)
         acc = [psum.tile([P, M], F32, name="acc%d" % h) for h in range(HALVES)]
-        result = [held.tile([P, M], F32, name="result%d" % h) for h in range(HALVES)]
+        result = [held.tile([P, M], F32, name="result%d" % h, offset=MX_AT + 31 * KIB + 512 * h) for h in range(HALVES)]
 
         width = (2 * BLOCKS + PASSES) * P
-        grouped = held.tile([P, width * PACK], BF16, name="grouped", align_bytes=64)
-        codes = held.tile([P, width], U32, name="codes", align_bytes=64)
-        scales = held.tile([P, width], U8, name="scales", align_bytes=64)
+        grouped = held.tile([P, width * PACK], BF16, name="grouped", align_bytes=64, offset=MX_AT)
+        codes = held.tile([P, width], U32, name="codes", align_bytes=64, offset=MX_AT + 18 * KIB)
+        scales = held.tile([P, width], U8, name="scales", align_bytes=64, offset=MX_AT + 27 * KIB)
         fours = grouped[:].rearrange("p (m i) -> p m i", i=PACK)
         w_at = [0, (BLOCKS + 1) * P]
         raw_at = 12 * P * PACK // 2
         w_raw = grouped[:].bitcast(F32)[:, raw_at : raw_at + PASSES * PACK * M].rearrange("p (a i n) -> p a i n", a=PASSES, i=PACK)
         first_at = PICKS + (PICKS - CUT_B) - P
-        staged = held.tile([P, 2 * first_at + CUT_B], F32, name="staged")
+        staged = held.tile([P, 2 * first_at + CUT_B], F32, name="staged", offset=STAGE_AT + 5 * KIB)
 
         def column_of(a, b):
             return (1 + (BLOCKS + 1) * a + b) * P
@@ -85,14 +88,14 @@ def tile_list_hbag_tm_res_kernel(tc, xT, w, wgt, r, offs, out):
                 nc.sync.dma_start(offsets[:], offs)
         nc.sync.dma_start(r_sb[:], r.rearrange("(h p) n -> p h n", p=P))
 
-        turned = held.tile([P, 2, SQ], F32, name="turned", align_bytes=64)
+        turned = held.tile([P, 2, SQ], F32, name="turned", align_bytes=64, offset=STAGE_AT + 4 * KIB + 512)
         for e in range(2):
             nc.vector.transpose(turned[:, e, :], wgt_rows[:, e * SQ : (e + 1) * SQ])
         by_run = turned[:].rearrange("j e (h b) -> j b (e h)", h=2)
         runs = LIST_ROWS // WGT_PARTS
         wides = []
         for j in range(WGT_PARTS):
-            wide = held.tile([P, runs, 4, LIST_ROWS], F32, name="wide%d" % j, align_bytes=64)
+            wide = held.tile([P, runs, 4, LIST_ROWS], F32, name="wide%d" % j, align_bytes=64, offset=MX_AT + (32 + j) * KIB)
             nc.vector.tensor_copy(wide[:], by_run[:, j * runs : (j + 1) * runs, :].unsqueeze(3).to_broadcast([P, runs, 4, LIST_ROWS]))
             wides.append(wide)
         for j in range(WGT_PARTS):

@@ -44,17 +44,17 @@ def tile_list_hbag_tm_res_kernel(tc, xT, w, wgt, r, offs, out):
         wgt_rows = held.tile([P, 2 * SQ], F32, name="wgt_rows", align_bytes=64, offset=STAGE_AT + 4 * KIB)
         planes = [held.tile([P, T], F32, name="plane%d" % q, offset=(ODD_AT if q % 2 else EVEN_AT) + q // 2 * 8 * KIB) for q in range(PLANES)]
         picked = [held.tile([P, 2, PICKS], F32, name="picked%d" % u, offset=STAGE_AT + (20 + 8 * u) * KIB) for u in range(3)]
-        r_sb = held.tile([P, HALVES, M], F32, name="r_sb", offset=MX_AT + 30 * KIB)
+        r_sb = held.tile([P, HALVES, M], F32, name="r_sb", offset=MX_AT + 31 * KIB)
         acc = [psum.tile([P, M], F32, name="acc%d" % h) for h in range(HALVES)]
-        result = [held.tile([P, M], F32, name="result%d" % h, offset=MX_AT + 31 * KIB + 512 * h) for h in range(HALVES)]
+        result = [held.tile([P, M], F32, name="result%d" % h, offset=MX_AT + 32 * KIB + 512 * h) for h in range(HALVES)]
 
         width = (2 * BLOCKS + PASSES) * P
-        grouped = held.tile([P, width * PACK], BF16, name="grouped", align_bytes=64, offset=MX_AT)
-        codes = held.tile([P, width], U32, name="codes", align_bytes=64, offset=MX_AT + 18 * KIB)
-        scales = held.tile([P, width], U8, name="scales", align_bytes=64, offset=MX_AT + 27 * KIB)
+        grouped = held.tile([P, (width + P) * PACK], BF16, name="grouped", align_bytes=64, offset=MX_AT)
+        codes = held.tile([P, width], U32, name="codes", align_bytes=64, offset=MX_AT + 19 * KIB)
+        scales = held.tile([P, width], U8, name="scales", align_bytes=64, offset=MX_AT + 28 * KIB)
         fours = grouped[:].rearrange("p (m i) -> p m i", i=PACK)
         w_at = [0, (BLOCKS + 1) * P]
-        raw_at = 12 * P * PACK // 2
+        raw_at = 15 * P * PACK // 2
         w_raw = grouped[:].bitcast(F32)[:, raw_at : raw_at + PASSES * PACK * M].rearrange("p (a i n) -> p a i n", a=PASSES, i=PACK)
         first_at = PICKS + (PICKS - CUT_B) - P
         staged = held.tile([P, 2 * first_at + CUT_B], F32, name="staged", offset=STAGE_AT + 5 * KIB)
@@ -95,7 +95,7 @@ def tile_list_hbag_tm_res_kernel(tc, xT, w, wgt, r, offs, out):
         runs = LIST_ROWS // WGT_PARTS
         wides = []
         for j in range(WGT_PARTS):
-            wide = held.tile([P, runs, 4, LIST_ROWS], F32, name="wide%d" % j, align_bytes=64, offset=MX_AT + (32 + j) * KIB)
+            wide = held.tile([P, runs, 4, LIST_ROWS], F32, name="wide%d" % j, align_bytes=64, offset=MX_AT + (33 + j) * KIB)
             nc.vector.tensor_copy(wide[:], by_run[:, j * runs : (j + 1) * runs, :].unsqueeze(3).to_broadcast([P, runs, 4, LIST_ROWS]))
             wides.append(wide)
         for j in range(WGT_PARTS):

@@ -86,7 +86,9 @@ def tile_list_hbag_tm_res_kernel(tc, xT, w, wgt, r, offs, out):
             nc.sync.dma_start(planes[q][:], x_rows[q // PACK, q % PACK])
             if q == 0:
                 nc.sync.dma_start(offsets[:], offs)
-        nc.sync.dma_start(r_sb[:], r.rearrange("(h p) n -> p h n", p=P))
+        r_rows = r.rearrange("(h p) n -> p h n", p=P)
+        for n0 in range(0, M, M // 2):
+            nc.sync.dma_start(r_sb[:, :, n0 : n0 + M // 2], r_rows[:, :, n0 : n0 + M // 2])
 
         turned = held.tile([P, 2, SQ], F32, name="turned", align_bytes=64, offset=STAGE_AT + 4 * KIB + 512)
         for e in range(2):

@@ -87,8 +87,8 @@ def tile_list_hbag_tm_res_kernel(tc, xT, w, wgt, r, offs, out):
             if q == 0:
                 nc.sync.dma_start(offsets[:], offs)
         r_rows = r.rearrange("(h p) n -> p h n", p=P)
-        for n0 in range(0, M, M // 2):
-            nc.sync.dma_start(r_sb[:, :, n0 : n0 + M // 2], r_rows[:, :, n0 : n0 + M // 2])
+        for n0, n1 in ((0, M // 2), (M // 2, 3 * M // 4), (3 * M // 4, M)):
+            nc.sync.dma_start(r_sb[:, :, n0:n1], r_rows[:, :, n0:n1])
 
         turned = held.tile([P, 2, SQ], F32, name="turned", align_bytes=64, offset=STAGE_AT + 4 * KIB + 512)
         for e in range(2):

@@ -98,17 +98,21 @@ def tile_list_hbag_tm_res_kernel(tc, xT, w, wgt, r, offs, out):
         wides = []
         for j in range(WGT_PARTS):
             wide = held.tile([P, runs, 4, LIST_ROWS], F32, name="wide%d" % j, align_bytes=64, offset=MX_AT + (33 + j) * KIB)
-            nc.vector.tensor_copy(wide[:], by_run[:, j * runs : (j + 1) * runs, :].unsqueeze(3).to_broadcast([P, runs, 4, LIST_ROWS]))
+            widen = nc.vector.tensor_copy if j < WGT_PARTS // 2 else nc.scalar.copy
+            widen(wide[:], by_run[:, j * runs : (j + 1) * runs, :].unsqueeze(3).to_broadcast([P, runs, 4, LIST_ROWS]))
             wides.append(wide)
         for j in range(WGT_PARTS):
             part = PICKS // WGT_PARTS
             nc.vector.transpose(wgt_sb[:, j * part : (j + 1) * part], wides[j][:].rearrange("j b y x -> j (b y x)"))
 
+        wgt_last = held.tile([P, PICKS - CUT_B], F32, name="wgt_last", offset=MX_AT + 37 * KIB)
+        nc.vector.tensor_copy(wgt_last[:], wgt_sb[:, CUT_B:])
+
         def gather(q, lo, hi):
             nc.vector.tensor_tensor(
                 products(q, lo, hi),
                 planes[q][:].indirect(offsets[:, lo // LIST_ROWS : hi // LIST_ROWS]),
-                wgt_sb[:, lo:hi],
+                wgt_last[:] if lo == CUT_B else wgt_sb[:, lo:hi],
                 MULT,
             )
 

from contextlib import ExitStack

import concourse.mybir as mybir

G, K, M, T, S = 4, 1024, 128, 2048, 256
FLOPS = 2 * K * G * S * M

F32 = mybir.dt.float32
BF16 = mybir.dt.bfloat16
U32 = mybir.dt.uint32
U16 = mybir.dt.uint16
U8 = mybir.dt.uint8
FP8X4 = mybir.dt.float8_e4m3fn_x4
MULT = mybir.AluOpType.mult
ADD = mybir.AluOpType.add

P = 128
PACK = 4
PASSES = K // (P * PACK)
PLANES = PASSES * PACK
PICKS = G * S
LIST_ROWS = 16
LISTS = P // LIST_ROWS
BLOCKS = PICKS // P
HALVES = S // P

SQ = 32
WGT_PARTS = 4
PLANES_BEFORE_W = 6
KIB = 1024
EVEN_AT, STAGE_AT, ODD_AT, MX_AT = 0, 64 * KIB, 128 * KIB, 192 * KIB
CUT_A, CUT_B = 320, 768


def tile_list_hbag_tm_res_kernel(tc, xT, w, wgt, r, offs, out):
    nc = tc.nc
    with ExitStack() as ctx:
        lists = ctx.enter_context(tc.tile_pool(name="lists", bufs=1))
        held = ctx.enter_context(tc.tile_pool(name="held", bufs=1))
        psum = ctx.enter_context(tc.psum_pool(name="psum", bufs=1))

        offsets = lists.tile([P, PICKS // LIST_ROWS], U16, name="offsets")
        wgt_sb = held.tile([P, PICKS], F32, name="wgt_sb", align_bytes=64, offset=STAGE_AT)
        wgt_rows = held.tile([P, 2 * SQ], F32, name="wgt_rows", align_bytes=64, offset=STAGE_AT + 4 * KIB)
        planes = [held.tile([P, T], F32, name="plane%d" % q, offset=(ODD_AT if q % 2 else EVEN_AT) + q // 2 * 8 * KIB) for q in range(PLANES)]
        picked = [held.tile([P, 2, PICKS], F32, name="picked%d" % u, offset=STAGE_AT + (20 + 8 * u) * KIB) for u in range(3)]
        r_sb = held.tile([P, HALVES, M], F32, name="r_sb", offset=MX_AT + 31 * KIB)
        acc = [psum.tile([P, M], F32, name="acc%d" % h) for h in range(HALVES)]
        result = [held.tile([P, M], F32, name="result%d" % h, offset=MX_AT + 32 * KIB + 512 * h) for h in range(HALVES)]

        width = (2 * BLOCKS + PASSES) * P
        grouped = held.tile([P, (width + P) * PACK], BF16, name="grouped", align_bytes=64, offset=MX_AT)
        codes = held.tile([P, width], U32, name="codes", align_bytes=64, offset=MX_AT + 19 * KIB)
        scales = held.tile([P, width], U8, name="scales", align_bytes=64, offset=MX_AT + 28 * KIB)
        fours = grouped[:].rearrange("p (m i) -> p m i", i=PACK)
        w_at = [0, (BLOCKS + 1) * P]
        raw_at = 15 * P * PACK // 2
        w_raw = grouped[:].bitcast(F32)[:, raw_at : raw_at + PASSES * PACK * M].rearrange("p (a i n) -> p a i n", a=PASSES, i=PACK)
        first_at = PICKS + (PICKS - CUT_B) - P
        staged = held.tile([P, 2 * first_at + CUT_B], F32, name="staged", offset=STAGE_AT + 5 * KIB)

        def column_of(a, b):
            return (1 + (BLOCKS + 1) * a + b) * P

        def column7(pick):
            return first_at + pick if pick < CUT_B else PICKS + pick - CUT_B

        def products(q, lo, hi):
            if q < 6:
                return picked[q // 2][:, q % 2, lo:hi]
            at = column7(lo) if q == 7 else lo
            return staged[:, at : at + hi - lo]

        def pairs(u, lo, hi):
            if u < 3:
                return picked[u][:, :, lo:hi].rearrange("p i m -> p m i")
            apart = column7(lo) - lo
            return staged[:, lo : lo + 2 * apart].rearrange("p (i m) -> p m i", i=2)[:, : hi - lo, :]

        x_rows = xT.rearrange("(a p i) t -> a i p t", p=P, i=PACK)
        half_rows = wgt.rearrange("p (e b c) -> (p e) b c", e=2, c=2 * SQ)
        nc.sync.dma_start(wgt_rows[:], half_rows[:: LIST_ROWS + 1])
        for q in range(PLANES):
            if q == PLANES_BEFORE_W:
                nc.sync.dma_start(w_raw, w.rearrange("(a p i) n -> p a i n", p=P, i=PACK))
            nc.sync.dma_start(planes[q][:], x_rows[q // PACK, q % PACK])
            if q == 0:
                nc.sync.dma_start(offsets[:], offs)
        r_rows = r.rearrange("(h p) n -> p h n", p=P)
        for n0, n1 in ((0, M // 2), (M // 2, 3 * M // 4), (3 * M // 4, M)):
            nc.sync.dma_start(r_sb[:, :, n0:n1], r_rows[:, :, n0:n1])

        turned = held.tile([P, 2, SQ], F32, name="turned", align_bytes=64, offset=STAGE_AT + 4 * KIB + 512)
        for e in range(2):
            nc.vector.transpose(turned[:, e, :], wgt_rows[:, e * SQ : (e + 1) * SQ])
        by_run = turned[:].rearrange("j e (h b) -> j b (e h)", h=2)
        runs = LIST_ROWS // WGT_PARTS
        wides = []
        for j in range(WGT_PARTS):
            wide = held.tile([P, runs, 4, LIST_ROWS], F32, name="wide%d" % j, align_bytes=64, offset=MX_AT + (33 + j) * KIB)
            widen = nc.vector.tensor_copy if j < WGT_PARTS // 2 else nc.scalar.copy
            widen(wide[:], by_run[:, j * runs : (j + 1) * runs, :].unsqueeze(3).to_broadcast([P, runs, 4, LIST_ROWS]))
            wides.append(wide)
        for j in range(WGT_PARTS):
            part = PICKS // WGT_PARTS
            nc.vector.transpose(wgt_sb[:, j * part : (j + 1) * part], wides[j][:].rearrange("j b y x -> j (b y x)"))

        wgt_last = held.tile([P, PICKS - CUT_B], F32, name="wgt_last", offset=MX_AT + 37 * KIB)
        nc.vector.tensor_copy(wgt_last[:], wgt_sb[:, CUT_B:])

        def gather(q, lo, hi):
            nc.vector.tensor_tensor(
                products(q, lo, hi),
                planes[q][:].indirect(offsets[:, lo // LIST_ROWS : hi // LIST_ROWS]),
                wgt_last[:] if lo == CUT_B else wgt_sb[:, lo:hi],
                MULT,
            )

        def interleave(u, lo, hi):
            a, i0 = u // 2, 2 * (u % 2)
            c0 = column_of(a, lo // P) + lo % P
            nc.scalar.copy(fours[:, c0 : c0 + hi - lo, i0 : i0 + 2], pairs(u, lo, hi))

        def interleave_w(a):
            nc.scalar.copy(
                fours[:, w_at[a] : w_at[a] + M, :].rearrange("p (n e) i -> p n i e", e=4),
                w_raw[:, a, :, :].rearrange("p i (n e) -> p n i e", e=4),
            )

        def quantize(lo, hi, to=None):
            to = lo if to is None else to
            nc.vector.quantize_mx(
                out=codes[:, to : to + hi - lo].bitcast(FP8X4),
                scales=scales[:, to : to + hi - lo],
                in_=grouped[:, lo * PACK : hi * PACK],
            )

        def codes_of(a, b):
            spent = [(0, 6), (0, 7), (1, 0), (0, 0), (1, 1)]
            return column_of(*spent[b - 1]) if a == 0 and 1 <= b <= 5 else column_of(a, b)

        def multiply(a, b):
            c0 = codes_of(a, b)
            nc.tensor.matmul_mx(
                out=acc[b % HALVES][:],
                lhsT=codes[:, c0 : c0 + P].bitcast(FP8X4),
                lhsT_scale=scales[:, c0 : c0 + P],
                rhs=codes[:, w_at[a] : w_at[a] + M].bitcast(FP8X4),
                rhs_scale=scales[:, w_at[a] : w_at[a] + M],
                start=(a, b) in ((0, 6), (0, 7)),
                stop=(a == 1 and b >= BLOCKS - HALVES),
            )

        for u in range(2):
            gather(2 * u, 0, PICKS)
            gather(2 * u + 1, 0, PICKS)
            interleave(u, 0, PICKS)
        gather(4, 0, PICKS)
        gather(5, 0, PICKS)
        for a in range(PASSES):
            interleave_w(a)
        interleave(2, 0, PICKS)
        quantize(0, 2 * P)
        gather(6, 0, PICKS)

        gather(7, 0, CUT_A)
        interleave(3, 0, P)
        interleave(3, P, CUT_A)
        gather(7, CUT_A, CUT_B)
        interleave(3, CUT_A, 4 * P)
        interleave(3, 4 * P, CUT_B)
        quantize(column_of(0, 6), column_of(1, 1))
        for a, b in ((0, 6), (0, 7), (1, 0), (0, 0)):
            multiply(a, b)
        gather(7, CUT_B, PICKS)
        for lo, hi in ((CUT_B, 7 * P), (7 * P, 7 * P + P // 2), (7 * P + P // 2, PICKS)):
            interleave(3, lo, hi)
        for a, b in ((1, 1), (1, 2), (1, 3), (0, 1), (0, 2), (0, 3), (0, 4), (1, 4), (1, 5), (1, 6), (0, 5)):
            quantize(column_of(a, b), column_of(a, b) + P, codes_of(a, b))
            multiply(a, b)
        quantize(column_of(1, 7), column_of(1, 7) + P // 2)
        quantize(column_of(1, 7) + P // 2, column_of(1, 7) + P)
        multiply(1, 7)

        for h in range(HALVES):
            nc.vector.tensor_tensor(result[h][:], acc[h][:], r_sb[:, h, :], ADD)
            nc.sync.dma_start(out[h * P : (h + 1) * P, :], result[h][:])
